import numpy as np
import ml_dtypes


def mxq(x, axis, fmt="e4m3"):
    dtype, down = {"e4m3": (ml_dtypes.float8_e4m3fn, 7), "e5m2": (ml_dtypes.float8_e5m2, 14)}[fmt]
    v = np.moveaxis(np.asarray(x, np.float32).astype(ml_dtypes.bfloat16).astype(np.float64), axis, -1)
    blocks = v.reshape(v.shape[:-1] + (-1, 32))
    amax = np.abs(blocks).max(-1, keepdims=True)
    byte = np.maximum(np.where(amax > 0, np.frexp(amax)[1] - 1 + 127, 0) - down, 1)
    scale = np.exp2(byte - 127.0)
    codes = (blocks / scale).astype(np.float32).astype(dtype).astype(np.float64)
    return np.moveaxis((codes * scale).reshape(v.shape), -1, axis)


WIDE = False


def mx_kscale(k):
    if not WIDE:
        return np.ones(k)
    levels = np.array([10, -10, 5, -5, 0])
    if k % 512:
        return np.exp2(np.random.permutation(np.resize(levels, k // 32))).repeat(32)
    a = np.empty((k // 512, 16))
    for p in range(k // 512):
        a[p, :8] = np.random.permutation(np.resize(levels, 8))
        for g in range(8):
            far = levels[np.abs(levels - a[p, g]) >= 10]
            a[p, g + 8] = far[np.random.randint(len(far))]
    return np.exp2(a.ravel()).repeat(32)


BF16 = ml_dtypes.bfloat16


def bf(x):
    return np.asarray(x, np.float32).astype(BF16)


def f64(x):
    return np.asarray(x).astype(np.float64)


E2M1 = np.array([0.0, 0.5, 1.0, 1.5, 2.0, 3.0, 4.0, 6.0, -0.0, -0.5, -1.0, -1.5, -2.0, -3.0, -4.0, -6.0])


def pack_weight(w, fmt):
    k, n = w.shape
    w = f64(bf(w)).reshape(k // 32, 32, n)
    amax = np.abs(w).max(1)
    if fmt == "e4m3":
        byte = np.frexp(amax)[1] - 1 + 127 - 7
    else:
        mant, ex = np.frexp(amax / 6.0)
        byte = np.where(mant > 0.5, ex, ex - 1) + 127
    byte = np.clip(np.where(amax > 0, byte, 1), 1, 254)
    scaled = (w * np.exp2(127.0 - byte)[:, None, :]).reshape(k, n).astype(np.float32)
    by_word = np.ascontiguousarray(scaled.reshape(k // 512, 128, 4, n).transpose(0, 1, 3, 2))
    if fmt == "e4m3":
        words = by_word.astype(ml_dtypes.float8_e4m3fn).view(np.uint8)
    else:
        c = by_word.astype(ml_dtypes.float4_e2m1fn).view(np.uint8) & 0xF
        words = c[..., 0::2] | (c[..., 1::2] << 4)
    return np.ascontiguousarray(words), np.ascontiguousarray(byte.astype(np.uint8).reshape(k // 512, 16, n))


def unpack_weight(words, scales, fmt):
    g, p, n, _ = words.shape
    if fmt == "e4m3":
        vals = np.ascontiguousarray(words).view(ml_dtypes.float8_e4m3fn).astype(np.float64)
    else:
        nib = np.empty((g, p, n, 4), np.uint8)
        nib[..., 0::2] = words & 0xF
        nib[..., 1::2] = words >> 4
        vals = E2M1[nib]
    vals = vals * np.repeat(np.exp2(scales.astype(np.float64) - 127.0), 8, axis=1)[..., None]
    return vals.transpose(0, 1, 3, 2).reshape(g * 512, n)
def pack4(w):
    words, scales = pack_weight(w, "e2m1")
    return words.reshape(words.shape[0], 128, -1), scales


def unpack4(words, scales):
    return unpack_weight(words.reshape(words.shape[0], 128, -1, 2), scales, "e2m1")


M, N, Q, P, C = 512, 1024, 1024, 1024, 2


def setup_inputs():
    s, r, t = mx_kscale(Q), mx_kscale(Q), mx_kscale(P)
    sxx = np.exp(0.2 * np.random.standard_normal(M))
    syy = np.exp(0.2 * np.random.standard_normal(M))
    sxy = 0.6 * np.tanh(np.random.standard_normal(M)) * np.sqrt(sxx * syy)
    det = sxx * syy - sxy * sxy
    win = np.random.standard_normal((Q, P)) / np.sqrt(Q) / P ** 0.25
    win_words, win_scales = pack4(win / r[:, None] / t)
    return {"tmpl": bf(np.random.standard_normal((M, Q)) * s),
            "dx": bf(np.random.standard_normal((Q, P)) / np.sqrt(Q) / P ** 0.25 / s[:, None] * t),
            "dy": bf(np.random.standard_normal((Q, P)) / np.sqrt(Q) / P ** 0.25 / s[:, None] * t),
            "inv": bf(np.stack([np.stack([syy, -sxy]), np.stack([-sxy, sxx])]) / det),
            "patch": bf(np.random.standard_normal((N, Q)) * r),
            "win_words": win_words,
            "win_scales": win_scales}


def reference(tmpl, dx, dy, inv, patch, win_words, win_scales):
    h = f64(inv)
    tq = mxq(f64(tmpl), 1, "e4m3")
    gx = tq @ mxq(f64(dx), 0, "e4m3")
    gy = tq @ mxq(f64(dy), 0, "e4m3")
    sd = h[0][:, :, None] * gx + h[1][:, :, None] * gy
    wf = mxq(f64(patch), 1, "e4m3") @ unpack4(win_words, win_scales)
    flow = mxq(sd.reshape(C * M, P), 1, "e4m3") @ mxq(wf, 1, "e4m3").T
    return flow.reshape(C, M, N)

@@ -1,0 +1,350 @@
+from contextlib import ExitStack
+
+import concourse.mybir as mybir
+from concourse.masks import make_identity
+
+M, N, Q, P, C = 512, 1024, 1024, 1024, 2
+FLOPS = 2 * M * Q * P * 2 + 2 * N * Q * P + 2 * C * M * P * N
+
+F32 = mybir.dt.float32
+BF16 = mybir.dt.bfloat16
+I32 = mybir.dt.int32
+U32 = mybir.dt.uint32
+U8 = mybir.dt.uint8
+FP8X4 = mybir.dt.float8_e4m3fn_x4
+FP4X4 = mybir.dt.float4_e2m1fn_x4
+MULT = mybir.AluOpType.mult
+ADD = mybir.AluOpType.add
+COPY = mybir.ActivationFunctionType.Copy
+
+BANKS = 8
+UNITS = [(0, 0, 0), (0, 0, 1), (0, 1, 0), (0, 1, 1), (1, 0, 0), (1, 0, 1), (1, 1, 0), (1, 1, 1)]
+RING_T = 6
+RING_ROW = 6
+RING_OUT = 8
+
+
+def orders():
+    sp = [("Lr", 0), ("Lr", 1), ("Lw", 0), ("Ls",), ("Ld", 0, 0, 0), ("Lw", 1), ("Lr", 2), ("Lr", 3), ("Ld", 0, 0, 1),
+        ("Lr", 4), ("Lr", 5), ("LD", 0, 1), ("Lr", 6), ("Lr", 7), ("LD", 1, 0), ("Lr", 8), ("Lr", 9), ("Lr", 10),
+        ("Lr", 11), ("LD", 1, 1), ("Li",), ("St", 0, 0, 0), ("St", 0, 0, 1), ("St", 0, 1, 0), ("St", 0, 1, 1),
+        ("St", 1, 0, 0), ("St", 1, 0, 1), ("St", 1, 1, 0), ("St", 1, 1, 1), ("St", 2, 0, 0), ("St", 2, 0, 1), ("St", 2, 1, 0),
+        ("St", 2, 1, 1), ("St", 3, 0, 0), ("St", 3, 0, 1), ("St", 3, 1, 0), ("St", 3, 1, 1)]
+    pe = [("T", 0), ("T", 1), ("WF", 0, 0), ("WF", 0, 1), ("WF", 1, 0), ("WF", 1, 1), ("T", 2), ("T", 3), ("T", 4),
+        ("T", 5), ("WF", 2, 0), ("WF", 2, 1), ("WF", 3, 0), ("WF", 3, 1), ("WF", 4, 0), ("WF", 4, 1), ("WF", 5, 0),
+        ("WF", 5, 1), ("T", 6), ("T", 7), ("T", 8), ("T", 9), ("WF", 6, 0), ("WF", 6, 1), ("WF", 7, 0), ("WF", 7, 1),
+        ("T", 10), ("T", 11), ("G", 0, 0, 0), ("G", 0, 0, 1), ("G", 0, 1, 0), ("G", 0, 1, 1), ("G", 1, 0, 0), ("G", 1, 0, 1),
+        ("G", 1, 1, 0), ("G", 1, 1, 1), ("TS", 0, 0), ("TS", 0, 1), ("G", 2, 0, 0), ("G", 2, 0, 1), ("G", 2, 1, 0),
+        ("G", 2, 1, 1), ("TS", 1, 0), ("TS", 1, 1), ("O", 0, 0, 0), ("O", 0, 0, 1), ("O", 0, 1, 0), ("O", 0, 1, 1),
+        ("G", 3, 0, 0), ("G", 3, 0, 1), ("G", 3, 1, 0), ("G", 3, 1, 1), ("TS", 2, 0), ("TS", 2, 1), ("O", 1, 0, 0),
+        ("O", 1, 0, 1), ("O", 1, 1, 0), ("O", 1, 1, 1), ("TS", 3, 0), ("TS", 3, 1), ("O", 2, 0, 0), ("O", 2, 0, 1),
+        ("O", 2, 1, 0), ("O", 2, 1, 1), ("O", 3, 0, 0), ("O", 3, 0, 1), ("O", 3, 1, 0), ("O", 3, 1, 1)]
+    act = [("CT", 0), ("CT", 1), ("CW", 0, 0), ("CW", 0, 1), ("CW", 1, 0), ("CW", 1, 1), ("CT", 2), ("CT", 4), ("CT", 5),
+        ("CW", 2, 0), ("CW", 2, 1), ("CW", 3, 0), ("CW", 3, 1), ("CW", 4, 0), ("CW", 4, 1), ("CW", 5, 0), ("CW", 5, 1),
+        ("CT", 6), ("CT", 7), ("CT", 8), ("CT", 9), ("CW", 6, 0), ("CW", 6, 1), ("CW", 7, 0), ("CW", 7, 1), ("CT", 10),
+        ("CT", 11), ("SC", 0, 0, 1), ("SC", 0, 0, 0), ("SC", 0, 1, 0), ("SC", 0, 1, 1), ("SC", 1, 0, 1), ("SC", 1, 0, 0),
+        ("SC", 1, 1, 1), ("SC", 1, 1, 0), ("CS", 0, 1), ("CS", 0, 0), ("SC", 2, 0, 0), ("SC", 2, 0, 1), ("SC", 2, 1, 1),
+        ("SC", 2, 1, 0), ("CO", 0, 0, 0), ("CS", 1, 0), ("CO", 0, 0, 1), ("CS", 1, 1), ("CO", 0, 1, 1), ("SC", 3, 0, 1),
+        ("SC", 3, 0, 0), ("SC", 3, 1, 1), ("SC", 3, 1, 0), ("CS", 2, 0), ("CO", 1, 0, 0), ("CO", 1, 0, 1), ("CO", 1, 1, 0),
+        ("CS", 3, 0), ("CO", 2, 0, 0), ("CO", 2, 1, 0), ("CO", 3, 0, 0), ("CO", 3, 1, 0)]
+    vec = [("Z",), ("WP", 0), ("QT", 0), ("I", 0, 0), ("WP", 1), ("QT", 1), ("I", 0, 1), ("QD", 0), ("I", 1, 0),
+        ("I", 1, 1), ("QD", 1), ("CT", 3), ("QT", 2), ("QT", 3), ("I", 2, 0), ("QT", 4), ("QT", 5), ("I", 2, 1),
+        ("I", 3, 1), ("QD", 2), ("I", 3, 0), ("I", 4, 0), ("I", 4, 1), ("QD", 3), ("QD", 4), ("I", 5, 0), ("I", 5, 1),
+        ("QT", 6), ("QT", 7), ("I", 6, 1), ("QT", 8), ("I", 6, 0), ("I", 7, 0), ("QD", 6), ("I", 7, 1), ("QD", 5),
+        ("QD", 7), ("QT", 9), ("Ci",), ("QT", 10), ("QW", 0, 0), ("QW", 0, 1), ("ST", 0, 0, 1), ("ST", 0, 0, 0),
+        ("ST", 0, 1, 0), ("ST", 0, 1, 1), ("ST", 1, 0, 1), ("ST", 1, 0, 0), ("ST", 1, 1, 1), ("ST", 1, 1, 0), ("QS", 0, 1),
+        ("QS", 0, 0), ("QW", 1, 0), ("QW", 1, 1), ("ST", 2, 0, 1), ("ST", 2, 0, 0), ("QT", 11), ("ST", 2, 1, 1),
+        ("ST", 2, 1, 0), ("QS", 1, 0), ("CO", 0, 1, 0), ("QS", 1, 1), ("ST", 3, 0, 1), ("ST", 3, 0, 0), ("CS", 2, 1),
+        ("ST", 3, 1, 1), ("ST", 3, 1, 0), ("QS", 2, 1), ("QS", 2, 0), ("CO", 1, 1, 1), ("CS", 3, 1), ("QS", 3, 0),
+        ("QS", 3, 1), ("CO", 2, 0, 1), ("CO", 2, 1, 1), ("CO", 3, 0, 1), ("CO", 3, 1, 1)]
+    return [[("Id",)], sp, pe, act, vec]
+
+
+def tile_lucas_kanade_flow_s11_kernel(tc, tmpl, dx, dy, inv, patch, win_words, win_scales, out):
+    nc = tc.nc
+    with ExitStack() as ctx:
+        keep = ctx.enter_context(tc.tile_pool(name="keep", bufs=1))
+        psum = ctx.enter_context(tc.psum_pool(name="psum", bufs=1))
+        ctx.enter_context(tc.manual_schedule())
+
+        def sb(name, shape, dtype, ring=None, bufs=1):
+            return keep.tile(shape, dtype, name=name, tag=ring or name, bufs=bufs, align_bytes=64)
+
+        banks = [psum.tile([128, 512], F32, name="bank%d" % b) for b in range(BANKS)]
+        ident = sb("ident", [128, 128], F32)
+        inv_raw = sb("inv_raw", [128, 4, 4], BF16)
+        inv_f = sb("inv_f", [128, 16], F32)
+        w_raw = [sb("w_raw%d" % h, [128, 2048], U8) for h in range(2)]
+        w_codes = {(h, u): sb("w_codes%d%d" % (h, u), [128, 1024], U8) for h in range(2) for u in range(2)}
+        ws_raw = sb("ws_raw", [128, 2048], U8)
+        w_scales = {(h, u): sb("w_scales%d%d" % (h, u), [128, 512], U8) for h in range(2) for u in range(2)}
+        row_raw = [sb("row_raw%d" % r, [128, 1024], BF16) for r in range(12)]
+        row_codes = [sb("row_codes%d" % r, [128, 256], U32) for r in range(12)]
+        row_scales = [sb("row_scales%d" % r, [128, 256], U8) for r in range(12)]
+        d_codes = {k: sb("d_codes%d%d%d" % k, [128, 512], U32) for k in UNITS}
+        d_scales = {k: sb("d_scales%d%d%d" % k, [128, 512], U8) for k in UNITS}
+        pairs = [(a, b) for a in range(2) for b in range(2)]
+        wf_bf = {k: sb("wf_bf%d%d" % k, [128, 2048], BF16) for k in pairs}
+        wf_codes = {k: sb("wf_codes%d%d" % k, [128, 512], U32) for k in pairs}
+        wf_scales = {k: sb("wf_scales%d%d" % k, [128, 512], U8) for k in pairs}
+        halves = [(i, s) for i in range(4) for s in range(2)]
+        sd_t = {k: sb("sd_t%d%d" % k, [128, 1024], BF16) for k in halves}
+        sd_codes = {k: sb("sd_codes%d%d" % k, [128, 256], U32) for k in halves}
+        sd_scales = {k: sb("sd_scales%d%d" % k, [128, 256], U8) for k in halves}
+        sd = {(i, s, c): sb("sd%d%d%d" % (i, s, c), [128, 512], BF16) for (i, s) in halves for c in range(2)}
+        live = {}
+        filters = (dx, dy)
+        tmpl_rows = tmpl.rearrange("(p i) k -> p i k", i=4)
+        out_rows = [out[c].rearrange("(p i) n -> p i n", i=4) for c in range(C)]
+
+        queues = orders()
+        bank_of = {}
+        freed_by = {}
+        needs_bank = {}
+        turn = 0
+        for s in queues[2]:
+            if s[0] == "G":
+                readers = [[("SC" if s[3] == 0 else "ST", s[1], s[2], c) for c in range(2)]]
+            else:
+                readers = [[({"T": "CT", "WF": "CW", "TS": "CS", "O": "CO"}[s[0]],) + s[1:]]]
+            bank_of[s] = []
+            needs_bank[s] = []
+            for rd in readers:
+                bank_of[s].append(banks[turn % BANKS])
+                needs_bank[s] += freed_by.get(turn % BANKS, [])
+                freed_by[turn % BANKS] = rd
+                turn += 1
+
+        def ring_needs(kind, queue, size, freer):
+            mine = [s for s in queue if s[0] == kind]
+            return {s: [freer(mine[j - size])] for j, s in enumerate(mine) if j >= size}
+
+        ring = {}
+        for part in (ring_needs("CT", [("CT", s[1]) for s in queues[2] if s[0] == "T"], RING_ROW, lambda s: ("QT", s[1])),
+                     ring_needs("SC", queues[3], RING_T, lambda s: ("ST",) + s[1:])):
+            for key in part:
+                ring[key] = part[key]
+        stores = [s for s in queues[1] if s[0] == "St"]
+        for j, s in enumerate(stores):
+            if j >= RING_OUT:
+                ring[("CO",) + s[1:]] = [stores[j - RING_OUT]]
+
+        def d_load(k):
+            a, g, s = UNITS[k]
+            return ("Ld", a, g, s) if ("Ld", a, g, s) in queues[1] else ("LD", a, g)
+
+        def needs(s):
+            kind = s[0]
+            base = needs_bank.get(s, []) + ring.get(s, [])
+            if kind == "Ls":
+                return [("Z",)]
+            if kind == "Ci":
+                return [("Li",)]
+            if kind == "T":
+                return base + [("Lr", s[1]), ("Id",)]
+            if kind == "CT":
+                return base + [("T", s[1])]
+            if kind == "QT":
+                return [("CT", s[1])]
+            if kind == "WP":
+                return [("Lw", s[1]), ("Ls",)]
+            if kind == "WF":
+                return base + [("WP", s[2]), ("QT", s[1])]
+            if kind == "CW":
+                return [("WF",) + s[1:]]
+            if kind == "QW":
+                return [("CW", 4 * s[1] + j, s[2]) for j in range(4)]
+            if kind == "I":
+                return [d_load(s[1])]
+            if kind == "QD":
+                return [("I", s[1], 0), ("I", s[1], 1)]
+            if kind == "G":
+                return base + [("QT", 8 + s[1])] + [("QD", UNITS.index((s[3], g, s[2]))) for g in range(2)]
+            if kind == "SC":
+                return base + [("G", s[1], s[2], 0), ("Ci",)]
+            if kind == "ST":
+                return [("SC",) + s[1:], ("G", s[1], s[2], 1)]
+            if kind == "TS":
+                return base + [("ST",) + s[1:] + (c,) for c in range(2)]
+            if kind == "CS":
+                return [("TS",) + s[1:]]
+            if kind == "QS":
+                return [("CS",) + s[1:]]
+            if kind == "O":
+                return base + [("QS", s[1], 0), ("QS", s[1], 1), ("QW", s[3], 0), ("QW", s[3], 1)]
+            if kind == "CO":
+                return base + [("O",) + s[1:]]
+            if kind == "St":
+                return [("CO",) + s[1:]]
+            return []
+
+        def emit(s, engine):
+            kind = s[0]
+            if kind == "Z":
+                nc.vector.memset(ws_raw[:].bitcast(I32), 0)
+            elif kind == "Id":
+                make_identity(nc, ident[:])
+            elif kind == "Li":
+                nc.sync.dma_start(out=inv_raw[:], in_=inv.rearrange("a c (p i) -> p (a c) i", i=4))
+            elif kind == "Ls":
+                for q in range(4):
+                    nc.sync.dma_start(
+                        out=ws_raw[32 * q : 32 * q + 4, :].bitcast(I32).rearrange("r (g n) -> r g n", g=2),
+                        in_=win_scales[:, 4 * q : 4 * q + 4, :].rearrange("g r n -> r g n").bitcast(I32))
+            elif kind == "Ci":
+                nc.vector.tensor_copy(out=inv_f[:], in_=inv_raw[:].rearrange("p a i -> p (a i)"))
+            elif kind == "Lw":
+                h = s[1]
+                nc.sync.dma_start(out=w_raw[h][:].bitcast(I32).rearrange("p (g n) -> p g n", g=2),
+                                  in_=win_words[:, :, 1024 * h : 1024 * (h + 1)].rearrange("g p b -> p g b").bitcast(I32))
+            elif kind == "Lr":
+                r = s[1]
+                src = patch[128 * r : 128 * (r + 1), :] if r < 8 else tmpl_rows[:, r - 8, :]
+                nc.sync.dma_start(out=row_raw[r][:], in_=src)
+            elif kind == "LD":
+                a, g = s[1:]
+                raw = sb("d_raw%d%d" % (a, g), [128, 4, 1024], BF16)
+                for h in range(2):
+                    live["raw", a, g, h] = raw[:, :, 512 * h : 512 * (h + 1)]
+                nc.sync.dma_start(out=raw[:], in_=filters[a][512 * g : 512 * (g + 1), :].rearrange("(p j) n -> p j n", j=4))
+            elif kind == "Ld":
+                a, g, h = s[1:]
+                cols = slice(512 * h, 512 * (h + 1))
+                raw = sb("d_raw%d%d%d" % (a, g, h), [128, 4, 512], BF16)
+                live["raw", a, g, h] = raw[:]
+                nc.sync.dma_start(out=raw[:],
+                                  in_=filters[a][512 * g : 512 * (g + 1), cols].rearrange("(p j) n -> p j n", j=4))
+            elif kind == "T":
+                words = row_raw[s[1]][:].bitcast(F32)
+                bank = bank_of[s][0]
+                for g in range(2):
+                    for u in range(2):
+                        j = 2 * g + u
+                        nc.tensor.transpose(bank[:, 128 * j : 128 * (j + 1)], words[:, 256 * g + u : 256 * (g + 1) : 2], ident[:])
+            elif kind == "CT":
+                live[s] = sb("row_t%d" % s[1], [128, 1024], BF16, ring="row_t", bufs=RING_ROW)
+                dst = live[s][:].bitcast(F32).rearrange("p (g r u) -> p g r u", g=2, u=2)
+                src = bank_of["T", s[1]][0][:].rearrange("p (g u r) -> p g r u", g=2, u=2)
+                if engine == 3:
+                    nc.scalar.copy(out=dst, in_=src)
+                else:
+                    nc.vector.tensor_copy(out=dst, in_=src)
+            elif kind == "QT":
+                nc.vector.quantize_mx(out=row_codes[s[1]][:].bitcast(FP8X4), scales=row_scales[s[1]][:], in_=live["CT", s[1]][:])
+            elif kind == "WP":
+                h = s[1]
+                for u in range(2):
+                    nc.vector.tensor_copy(
+                        out=w_scales[h, u][:].bitcast(I32).rearrange("p (g e b) -> p g e b", g=2, e=2),
+                        in_=ws_raw[:].bitcast(I32).rearrange("p (g h b e u) -> p h u g e b", g=2, h=2, e=2, u=2)[:, h, u])
+                    nc.vector.tensor_copy(
+                        out=w_codes[h, u][:].bitcast(I32).rearrange("p (g e b w) -> p g e b w", g=2, e=2, w=2),
+                        in_=w_raw[h][:].bitcast(I32).rearrange("p (g b e u w) -> p u g e b w", g=2, e=2, u=2, w=2)[:, u])
+            elif kind == "WF":
+                n, h = s[1:]
+                bank = bank_of[s][0]
+                for t in range(4):
+                    for g in range(2):
+                        u, x = t // 2, 2 * g + t % 2
+                        nc.tensor.matmul_mx(
+                            out=bank[:, 128 * t : 128 * (t + 1)],
+                            lhsT=w_codes[h, u][:, 256 * x : 256 * (x + 1)].bitcast(FP4X4), lhsT_scale=w_scales[h, u][:, 128 * x : 128 * (x + 1)],
+                            rhs=row_codes[n][:, 128 * g : 128 * (g + 1)].bitcast(FP8X4), rhs_scale=row_scales[n][:, 128 * g : 128 * (g + 1)],
+                            start=(g == 0), stop=(g == 1))
+            elif kind == "CW":
+                n, h = s[1:]
+                dst = wf_bf[n // 4, h][:, 512 * (n % 4) : 512 * (n % 4 + 1)].rearrange("p (r t) -> p r t", t=4)
+                src = bank_of["WF", n, h][0][:].rearrange("p (t r) -> p r t", t=4)
+                if engine == 3:
+                    nc.scalar.activation(out=dst, in_=src, func=COPY)
+                else:
+                    nc.vector.tensor_copy(out=dst, in_=src)
+            elif kind == "QW":
+                k = s[1:]
+                nc.vector.quantize_mx(out=wf_codes[k][:].bitcast(FP8X4), scales=wf_scales[k][:], in_=wf_bf[k][:])
+            elif kind == "I":
+                k, e = s[1:]
+                a, g, h = UNITS[k]
+                if ("D", k) not in live:
+                    live["D", k] = sb("d_t%d" % k, [128, 2048], BF16, ring="d_t", bufs=3)
+                dst = live["D", k][:].rearrange("p (e u b i j) -> p e b u j i", e=2, u=2, i=4, j=4)[:, e]
+                src = live["raw", a, g, h].rearrange("p j (b e u i) -> p e b u j i", u=2, e=2, i=4)[:, e]
+                if engine == 3:
+                    nc.scalar.copy(out=dst, in_=src)
+                else:
+                    nc.vector.tensor_copy(out=dst, in_=src)
+            elif kind == "QD":
+                k = UNITS[s[1]]
+                nc.vector.quantize_mx(out=d_codes[k][:].bitcast(FP8X4), scales=d_scales[k][:], in_=live["D", s[1]][:])
+            elif kind == "G":
+                i, h, a = s[1:]
+                if True:
+                    for g in range(2):
+                        nc.tensor.matmul_mx(
+                            out=bank_of[s][0][:],
+                            lhsT=row_codes[8 + i][:, 128 * g : 128 * (g + 1)].bitcast(FP8X4),
+                            lhsT_scale=row_scales[8 + i][:, 128 * g : 128 * (g + 1)],
+                            rhs=d_codes[a, g, h][:].bitcast(FP8X4), rhs_scale=d_scales[a, g, h][:],
+                            start=(g == 0), stop=(g == 1))
+            elif kind == "SC":
+                i, h, c = s[1:]
+                live[s] = sb("gx_part%d%d%d" % s[1:], [128, 512], F32, ring="gx_part", bufs=RING_T)
+                nc.scalar.activation(out=live[s][:].rearrange("p (x e) -> p x e", e=2),
+                                     in_=bank_of["G", i, h, 0][0][:].rearrange("p (e x) -> p x e", e=2),
+                                     func=COPY, scale=inv_f[:, 4 * c + i : 4 * c + i + 1])
+            elif kind == "ST":
+                i, h, c = s[1:]
+                nc.vector.scalar_tensor_tensor(
+                    out=sd[i, h, c][:].rearrange("p (x e) -> p x e", e=2),
+                    in0=bank_of["G", i, h, 1][0][:].rearrange("p (e x) -> p x e", e=2),
+                    scalar=inv_f[:, 8 + 4 * c + i : 8 + 4 * c + i + 1],
+                    in1=live["SC", i, h, c][:].rearrange("p (x e) -> p x e", e=2), op0=MULT, op1=ADD)
+            elif kind == "TS":
+                i, h = s[1:]
+                for c in range(2):
+                    words = sd[i, h, c][:].bitcast(F32)
+                    for u in range(2):
+                        j = 2 * c + u
+                        nc.tensor.transpose(bank_of[s][0][:, 128 * j : 128 * (j + 1)], words[:, 128 * u : 128 * (u + 1)], ident[:])
+            elif kind == "CS":
+                k = s[1:]
+                dst = sd_t[k][:].bitcast(F32).rearrange("p (c r u) -> p c r u", c=2, u=2)
+                src = bank_of[("TS",) + k][0][:].rearrange("p (c u r) -> p c r u", c=2, u=2)
+                if engine == 3:
+                    nc.scalar.copy(out=dst, in_=src)
+                else:
+                    nc.vector.tensor_copy(out=dst, in_=src)
+            elif kind == "QS":
+                k = s[1:]
+                nc.vector.quantize_mx(out=sd_codes[k][:].bitcast(FP8X4), scales=sd_scales[k][:], in_=sd_t[k][:])
+            elif kind == "O":
+                i, c, h = s[1:]
+                for g in range(2):
+                    nc.tensor.matmul_mx(
+                        out=bank_of[s][0][:],
+                        lhsT=sd_codes[i, g][:, 128 * c : 128 * (c + 1)].bitcast(FP8X4), lhsT_scale=sd_scales[i, g][:, 128 * c : 128 * (c + 1)],
+                        rhs=wf_codes[h, g][:].bitcast(FP8X4), rhs_scale=wf_scales[h, g][:],
+                        start=(g == 0), stop=(g == 1))
+            elif kind == "CO":
+                i, c, h = s[1:]
+                live[s] = sb("res%d%d%d" % (i, c, h), [128, 512], F32, ring="res", bufs=RING_OUT)
+                dst = live[s][:]
+                if engine == 3:
+                    nc.scalar.copy(out=dst, in_=bank_of["O", i, c, h][0][:])
+                else:
+                    nc.vector.tensor_copy(out=dst, in_=bank_of["O", i, c, h][0][:])
+            elif kind == "St":
+                i, c, h = s[1:]
+                nc.sync.dma_start(out=out_rows[c][:, i, 512 * h : 512 * (h + 1)], in_=live["CO", i, c, h][:])
+
+        done = set()
+        at = [0] * len(queues)
+        total = sum(len(q) for q in queues)
+        while len(done) < total:
+            before = len(done)
+            for e, queue in enumerate(queues):
+                while at[e] < len(queue) and all(n in done for n in needs(queue[at[e]])):
+                    emit(queue[at[e]], e)
+                    done.add(queue[at[e]])
+                    at[e] += 1
+            assert len(done) > before

@@ -18,45 +18,47 @@ ADD = mybir.AluOpType.add
 COPY = mybir.ActivationFunctionType.Copy
 
 BANKS = 8
+WARM = 8
 UNITS = [(0, 0, 0), (0, 0, 1), (0, 1, 0), (0, 1, 1), (1, 0, 0), (1, 0, 1), (1, 1, 0), (1, 1, 1)]
+GROUPS = [(0,), (1,), (2, 3), (4, 5), (6, 7), (8, 9), (10, 11)]
+GROUP_OF = {r: (x, j) for x, rows in enumerate(GROUPS) for j, r in enumerate(rows)}
 RING_T = 6
-RING_ROW = 6
-RING_OUT = 8
+RING_ROW = 3
+RING_OUT = 5
 
 
 def orders():
-    sp = [("Lr", 0), ("Lr", 1), ("Lw", 0), ("Ls",), ("Ld", 0, 0, 0), ("Lw", 1), ("Lr", 2), ("Lr", 3), ("Ld", 0, 0, 1),
-        ("Lr", 4), ("Lr", 5), ("LD", 0, 1), ("Lr", 6), ("Lr", 7), ("LD", 1, 0), ("Lr", 8), ("Lr", 9), ("Lr", 10),
-        ("Lr", 11), ("LD", 1, 1), ("Li",), ("St", 0, 0, 0), ("St", 0, 0, 1), ("St", 0, 1, 0), ("St", 0, 1, 1),
-        ("St", 1, 0, 0), ("St", 1, 0, 1), ("St", 1, 1, 0), ("St", 1, 1, 1), ("St", 2, 0, 0), ("St", 2, 0, 1), ("St", 2, 1, 0),
-        ("St", 2, 1, 1), ("St", 3, 0, 0), ("St", 3, 0, 1), ("St", 3, 1, 0), ("St", 3, 1, 1)]
-    pe = [("T", 0), ("T", 1), ("WF", 0, 0), ("WF", 0, 1), ("WF", 1, 0), ("WF", 1, 1), ("T", 2), ("T", 3), ("T", 4),
-        ("T", 5), ("WF", 2, 0), ("WF", 2, 1), ("WF", 3, 0), ("WF", 3, 1), ("WF", 4, 0), ("WF", 4, 1), ("WF", 5, 0),
-        ("WF", 5, 1), ("T", 6), ("T", 7), ("T", 8), ("T", 9), ("WF", 6, 0), ("WF", 6, 1), ("WF", 7, 0), ("WF", 7, 1),
-        ("T", 10), ("T", 11), ("G", 0, 0, 0), ("G", 0, 0, 1), ("G", 0, 1, 0), ("G", 0, 1, 1), ("G", 1, 0, 0), ("G", 1, 0, 1),
-        ("G", 1, 1, 0), ("G", 1, 1, 1), ("TS", 0, 0), ("TS", 0, 1), ("G", 2, 0, 0), ("G", 2, 0, 1), ("G", 2, 1, 0),
-        ("G", 2, 1, 1), ("TS", 1, 0), ("TS", 1, 1), ("O", 0, 0, 0), ("O", 0, 0, 1), ("O", 0, 1, 0), ("O", 0, 1, 1),
-        ("G", 3, 0, 0), ("G", 3, 0, 1), ("G", 3, 1, 0), ("G", 3, 1, 1), ("TS", 2, 0), ("TS", 2, 1), ("O", 1, 0, 0),
-        ("O", 1, 0, 1), ("O", 1, 1, 0), ("O", 1, 1, 1), ("TS", 3, 0), ("TS", 3, 1), ("O", 2, 0, 0), ("O", 2, 0, 1),
-        ("O", 2, 1, 0), ("O", 2, 1, 1), ("O", 3, 0, 0), ("O", 3, 0, 1), ("O", 3, 1, 0), ("O", 3, 1, 1)]
-    act = [("CT", 0), ("CT", 1), ("CW", 0, 0), ("CW", 0, 1), ("CW", 1, 0), ("CW", 1, 1), ("CT", 2), ("CT", 4), ("CT", 5),
-        ("CW", 2, 0), ("CW", 2, 1), ("CW", 3, 0), ("CW", 3, 1), ("CW", 4, 0), ("CW", 4, 1), ("CW", 5, 0), ("CW", 5, 1),
-        ("CT", 6), ("CT", 7), ("CT", 8), ("CT", 9), ("CW", 6, 0), ("CW", 6, 1), ("CW", 7, 0), ("CW", 7, 1), ("CT", 10),
-        ("CT", 11), ("SC", 0, 0, 1), ("SC", 0, 0, 0), ("SC", 0, 1, 0), ("SC", 0, 1, 1), ("SC", 1, 0, 1), ("SC", 1, 0, 0),
-        ("SC", 1, 1, 1), ("SC", 1, 1, 0), ("CS", 0, 1), ("CS", 0, 0), ("SC", 2, 0, 0), ("SC", 2, 0, 1), ("SC", 2, 1, 1),
-        ("SC", 2, 1, 0), ("CO", 0, 0, 0), ("CS", 1, 0), ("CO", 0, 0, 1), ("CS", 1, 1), ("CO", 0, 1, 1), ("SC", 3, 0, 1),
-        ("SC", 3, 0, 0), ("SC", 3, 1, 1), ("SC", 3, 1, 0), ("CS", 2, 0), ("CO", 1, 0, 0), ("CO", 1, 0, 1), ("CO", 1, 1, 0),
-        ("CS", 3, 0), ("CO", 2, 0, 0), ("CO", 2, 1, 0), ("CO", 3, 0, 0), ("CO", 3, 1, 0)]
-    vec = [("Z",), ("WP", 0), ("QT", 0), ("I", 0, 0), ("WP", 1), ("QT", 1), ("I", 0, 1), ("QD", 0), ("I", 1, 0),
-        ("I", 1, 1), ("QD", 1), ("CT", 3), ("QT", 2), ("QT", 3), ("I", 2, 0), ("QT", 4), ("QT", 5), ("I", 2, 1),
-        ("I", 3, 1), ("QD", 2), ("I", 3, 0), ("I", 4, 0), ("I", 4, 1), ("QD", 3), ("QD", 4), ("I", 5, 0), ("I", 5, 1),
-        ("QT", 6), ("QT", 7), ("I", 6, 1), ("QT", 8), ("I", 6, 0), ("I", 7, 0), ("QD", 6), ("I", 7, 1), ("QD", 5),
-        ("QD", 7), ("QT", 9), ("Ci",), ("QT", 10), ("QW", 0, 0), ("QW", 0, 1), ("ST", 0, 0, 1), ("ST", 0, 0, 0),
-        ("ST", 0, 1, 0), ("ST", 0, 1, 1), ("ST", 1, 0, 1), ("ST", 1, 0, 0), ("ST", 1, 1, 1), ("ST", 1, 1, 0), ("QS", 0, 1),
-        ("QS", 0, 0), ("QW", 1, 0), ("QW", 1, 1), ("ST", 2, 0, 1), ("ST", 2, 0, 0), ("QT", 11), ("ST", 2, 1, 1),
-        ("ST", 2, 1, 0), ("QS", 1, 0), ("CO", 0, 1, 0), ("QS", 1, 1), ("ST", 3, 0, 1), ("ST", 3, 0, 0), ("CS", 2, 1),
-        ("ST", 3, 1, 1), ("ST", 3, 1, 0), ("QS", 2, 1), ("QS", 2, 0), ("CO", 1, 1, 1), ("CS", 3, 1), ("QS", 3, 0),
-        ("QS", 3, 1), ("CO", 2, 0, 1), ("CO", 2, 1, 1), ("CO", 3, 0, 1), ("CO", 3, 1, 1)]
+    sp = [("Lr", 0), ("Lr", 1), ("Lp", 1), ("Ls",), ("Lw", 0), ("Lw", 1), ("Li",), ("LD", 0, 0), ("Ld", 0, 1, 0),
+        ("Lp", 2), ("Lp", 3), ("Ld", 0, 1, 1), ("Lp", 5), ("Ld", 1, 0, 0), ("Lp", 4), ("Ld", 1, 1, 0), ("Ld", 1, 0, 1),
+        ("Ld", 1, 1, 1), ("St", 0, 0, 0), ("St", 0, 1, 0), ("St", 0, 0, 1), ("St", 0, 1, 1), ("St", 1, 0, 0), ("St", 1, 0, 1),
+        ("St", 1, 1, 1), ("St", 2, 0, 0), ("St", 1, 1, 0), ("St", 2, 0, 1), ("St", 2, 1, 0), ("St", 2, 1, 1), ("St", 3, 1, 0),
+        ("St", 3, 1, 1), ("St", 3, 0, 0), ("St", 3, 0, 1, 0), ("St", 3, 0, 1, 1)]
+    pe = [("Wm",), ("T", 0), ("T", 1), ("T", 3), ("T", 2), ("WF", 0, 0), ("WF", 0, 1), ("WF", 1, 0), ("M", ("WF", 2, 0),
+        ("WF", 3, 0)), ("WF", 1, 1), ("T", 4), ("T", 5), ("M", ("WF", 2, 1), ("WF", 3, 1)), ("T", 7), ("T", 6),
+        ("T", 10), ("M", ("WF", 4, 0), ("WF", 5, 0)), ("T", 9), ("T", 8), ("T", 11), ("M", ("WF", 4, 1), ("WF", 5, 1)),
+        ("M", ("WF", 6, 0), ("WF", 7, 0)), ("M", ("WF", 6, 1), ("WF", 7, 1)), ("G", 0, 0, 0), ("G", 0, 0, 1), ("G", 0, 1, 0),
+        ("G", 1, 1, 0), ("G", 0, 1, 1), ("G", 1, 1, 1), ("G", 1, 0, 0), ("G", 1, 0, 1), ("G", 2, 0, 0), ("TS", 0, 0),
+        ("TS", 0, 1), ("TS", 1, 1), ("G", 2, 1, 0), ("TS", 1, 0), ("G", 2, 0, 1), ("G", 3, 0, 0), ("G", 2, 1, 1),
+        ("O", 0, 0, 0), ("O", 0, 1, 0), ("O", 0, 0, 1), ("G", 3, 1, 0), ("O", 0, 1, 1), ("TS", 2, 0), ("TS", 2, 1),
+        ("G", 3, 0, 1), ("G", 3, 1, 1), ("O", 1, 0, 0), ("O", 1, 0, 1), ("O", 1, 1, 0), ("O", 1, 1, 1), ("O", 2, 0, 0),
+        ("TS", 3, 0), ("TS", 3, 1), ("O", 2, 0, 1), ("O", 2, 1, 0), ("O", 2, 1, 1), ("O", 3, 1, 0), ("O", 3, 1, 1),
+        ("O", 3, 0, 0), ("O", 3, 0, 1, 0), ("O", 3, 0, 1, 1)]
+    act = [("Ci",), ("CT", 1), ("CT", 2), ("CW", 0, 0), ("CW", 0, 1), ("CW", 1, 0), ("I", 2), ("CW", 2, 0), ("CT", 5),
+        ("CT", 4), ("CW", 1, 1), ("CW", 2, 1), ("CT", 7), ("CT", 6), ("CT", 10), ("CW", 3, 1), ("CW", 5, 0), ("CT", 9),
+        ("CT", 8), ("CW", 4, 0), ("CT", 11), ("CW", 5, 1), ("CW", 4, 1), ("CW", 7, 0), ("CW", 6, 0), ("CW", 7, 1),
+        ("SC", 0, 0, 0), ("CW", 6, 1), ("SC", 0, 0, 1), ("SC", 0, 1, 1), ("SC", 0, 1, 0), ("SC", 1, 1, 0), ("SC", 1, 1, 1),
+        ("SC", 1, 0, 1), ("SC", 1, 0, 0), ("CS", 0, 0), ("SC", 2, 0, 0), ("CS", 0, 1), ("SC", 2, 0, 1), ("CS", 1, 1),
+        ("SC", 2, 1, 1), ("SC", 2, 1, 0), ("CS", 1, 0), ("SC", 3, 0, 0), ("SC", 3, 0, 1), ("SC", 3, 1, 1), ("CO", 0, 1, 0),
+        ("CS", 2, 1), ("SC", 3, 1, 0), ("CS", 2, 0), ("CO", 0, 1, 1), ("CO", 1, 0, 0), ("CO", 1, 0, 1), ("CO", 1, 1, 1),
+        ("CO", 1, 1, 0), ("CS", 3, 0), ("CO", 2, 0, 1), ("CO", 2, 1, 0), ("CO", 2, 1, 1), ("CO", 3, 1, 1), ("CO", 3, 0, 0),
+        ("CO", 3, 0, 1, 1)]
+    vec = [("Z",), ("CT", 0), ("QT", 0), ("WP", 0), ("WP", 1), ("CT", 3), ("QT", 1), ("QT", 2), ("I", 1), ("I", 0),
+        ("QD", 1), ("CW", 3, 0), ("QD", 0), ("QD", 2), ("I", 3), ("QT", 3), ("QD", 3), ("I", 4), ("QT", 4), ("QD", 4),
+        ("I", 6), ("QT", 5), ("QD", 6), ("I", 5), ("I", 7), ("QD", 5), ("QD", 7), ("ST", 0, 0, 0), ("QT", 6), ("ST", 0, 0, 1),
+        ("ST", 0, 1, 1), ("ST", 0, 1, 0), ("ST", 1, 1, 0), ("ST", 1, 1, 1), ("ST", 1, 0, 1), ("ST", 1, 0, 0), ("QW", 0),
+        ("QS", 0), ("QW", 1), ("ST", 2, 0, 1), ("ST", 2, 1, 1), ("ST", 2, 0, 0), ("ST", 2, 1, 0), ("CO", 0, 0, 0),
+        ("CO", 0, 0, 1), ("QS", 1), ("ST", 3, 0, 0), ("ST", 3, 1, 1), ("QS", 2), ("ST", 3, 0, 1), ("ST", 3, 1, 0),
+        ("CO", 2, 0, 0), ("CS", 3, 1), ("QS", 3), ("CO", 3, 1, 0), ("CO", 3, 0, 1, 0)]
     return [[("Id",)], sp, pe, act, vec]
 
 
@@ -74,24 +76,36 @@ def tile_lucas_kanade_flow_s11_kernel(tc, tmpl, dx, dy, inv, patch, win_words, w
         ident = sb("ident", [128, 128], F32)
         inv_raw = sb("inv_raw", [128, 4, 4], BF16)
         inv_f = sb("inv_f", [128, 16], F32)
-        w_raw = [sb("w_raw%d" % h, [128, 2048], U8) for h in range(2)]
-        w_codes = {(h, u): sb("w_codes%d%d" % (h, u), [128, 1024], U8) for h in range(2) for u in range(2)}
+        queues = orders()
+        if ("LW",) in queues[1]:
+            w_all = sb("w_all", [128, 4096], U8)
+            w_view = [w_all[:].bitcast(I32).rearrange("p (g h b f w) -> p h g f b w", g=2, h=2, f=4, w=2)[:, h] for h in range(2)]
+        else:
+            w_raw = [sb("w_raw%d" % h, [128, 2048], U8) for h in range(2)]
+            w_view = [w_raw[h][:].bitcast(I32).rearrange("p (g b f w) -> p g f b w", g=2, f=4, w=2) for h in range(2)]
+        w_codes = [sb("w_codes%d" % h, [128, 2048], U8) for h in range(2)]
         ws_raw = sb("ws_raw", [128, 2048], U8)
-        w_scales = {(h, u): sb("w_scales%d%d" % (h, u), [128, 512], U8) for h in range(2) for u in range(2)}
-        row_raw = [sb("row_raw%d" % r, [128, 1024], BF16) for r in range(12)]
-        row_codes = [sb("row_codes%d" % r, [128, 256], U32) for r in range(12)]
-        row_scales = [sb("row_scales%d" % r, [128, 256], U8) for r in range(12)]
+        w_scales = [sb("w_scales%d" % h, [128, 1024], U8) for h in range(2)]
+        patch_raw = [sb("patch_raw%d" % x, [128, 2, 1024], BF16) for x in range(4)]
+        tmpl_raw = sb("tmpl_raw", [128, 4, 1024], BF16)
+        row_raw = [patch_raw[r // 2][:, r % 2, :] if r < 8 else tmpl_raw[:, r - 8, :] for r in range(12)]
+        patch_rows = patch.rearrange("(x p j) k -> x p j k", x=4, j=2)
+        grp_codes = [sb("row_codes%d" % x, [128, 256 * len(rows)], U32) for x, rows in enumerate(GROUPS)]
+        grp_scales = [sb("row_scales%d" % x, [128, 256 * len(rows)], U8) for x, rows in enumerate(GROUPS)]
+        row_codes = [grp_codes[GROUP_OF[r][0]][:, 256 * GROUP_OF[r][1] : 256 * (GROUP_OF[r][1] + 1)] for r in range(12)]
+        row_scales = [grp_scales[GROUP_OF[r][0]][:, 256 * GROUP_OF[r][1] : 256 * (GROUP_OF[r][1] + 1)] for r in range(12)]
         d_codes = {k: sb("d_codes%d%d%d" % k, [128, 512], U32) for k in UNITS}
         d_scales = {k: sb("d_scales%d%d%d" % k, [128, 512], U8) for k in UNITS}
         pairs = [(a, b) for a in range(2) for b in range(2)]
-        wf_bf = {k: sb("wf_bf%d%d" % k, [128, 2048], BF16) for k in pairs}
-        wf_codes = {k: sb("wf_codes%d%d" % k, [128, 512], U32) for k in pairs}
-        wf_scales = {k: sb("wf_scales%d%d" % k, [128, 512], U8) for k in pairs}
+        wf_bf = [sb("wf_bf%d" % x, [128, 4096], BF16) for x in range(2)]
+        wf_codes = [sb("wf_codes%d" % x, [128, 1024], U32) for x in range(2)]
+        wf_scales = [sb("wf_scales%d" % x, [128, 1024], U8) for x in range(2)]
         halves = [(i, s) for i in range(4) for s in range(2)]
-        sd_t = {k: sb("sd_t%d%d" % k, [128, 1024], BF16) for k in halves}
-        sd_codes = {k: sb("sd_codes%d%d" % k, [128, 256], U32) for k in halves}
-        sd_scales = {k: sb("sd_scales%d%d" % k, [128, 256], U8) for k in halves}
+        sd_t = [sb("sd_t%d" % i, [128, 2048], BF16) for i in range(4)]
+        sd_codes = [sb("sd_codes%d" % i, [128, 512], U32) for i in range(4)]
+        sd_scales = [sb("sd_scales%d" % i, [128, 512], U8) for i in range(4)]
         sd = {(i, s, c): sb("sd%d%d%d" % (i, s, c), [128, 512], BF16) for (i, s) in halves for c in range(2)}
+        d_t = [sb("d_t%d" % k, [128, 2048], BF16) for k in range(3)]
         live = {}
         filters = (dx, dy)
         tmpl_rows = tmpl.rearrange("(p i) k -> p i k", i=4)
@@ -102,7 +116,8 @@ def tile_lucas_kanade_flow_s11_kernel(tc, tmpl, dx, dy, inv, patch, win_words, w
         freed_by = {}
         needs_bank = {}
         turn = 0
-        for s in queues[2]:
+        flat = [x for m in queues[2] for x in (m[1:] if m[0] == "M" else (m,)) if x[0] != "Wm"]
+        for s in flat:
             if s[0] == "G":
                 readers = [[("SC" if s[3] == 0 else "ST", s[1], s[2], c) for c in range(2)]]
             else:
@@ -119,15 +134,26 @@ def tile_lucas_kanade_flow_s11_kernel(tc, tmpl, dx, dy, inv, patch, win_words, w
             mine = [s for s in queue if s[0] == kind]
             return {s: [freer(mine[j - size])] for j, s in enumerate(mine) if j >= size}
 
+        used = []
+        for s in flat:
+            if s[0] == "T" and GROUP_OF[s[1]][0] not in used:
+                used.append(GROUP_OF[s[1]][0])
+        row_t = [sb("row_t%d" % k, [128, 2048], BF16) for k in range(RING_ROW)]
         ring = {}
-        for part in (ring_needs("CT", [("CT", s[1]) for s in queues[2] if s[0] == "T"], RING_ROW, lambda s: ("QT", s[1])),
+        for part in ({("CT", r): [("QT", used[used.index(GROUP_OF[r][0]) - RING_ROW])] for r in range(12) if used.index(GROUP_OF[r][0]) >= RING_ROW},
                      ring_needs("SC", queues[3], RING_T, lambda s: ("ST",) + s[1:])):
             for key in part:
                 ring[key] = part[key]
         stores = [s for s in queues[1] if s[0] == "St"]
-        for j, s in enumerate(stores):
-            if j >= RING_OUT:
-                ring[("CO",) + s[1:]] = [stores[j - RING_OUT]]
+        res = [sb("res%d" % k, [128, 1024], F32) for k in range(RING_OUT)]
+        rows_out = []
+        for s in flat:
+            if s[0] == "O" and s[1:3] not in rows_out:
+                rows_out.append(s[1:3])
+        for s in flat:
+            if s[0] == "O" and rows_out.index(s[1:3]) >= RING_OUT:
+                old = rows_out[rows_out.index(s[1:3]) - RING_OUT]
+                ring[("CO",) + s[1:]] = [x for x in stores if x[1:3] == old]
 
         def d_load(k):
             a, g, s = UNITS[k]
@@ -135,31 +161,36 @@ def tile_lucas_kanade_flow_s11_kernel(tc, tmpl, dx, dy, inv, patch, win_words, w
 
         def needs(s):
             kind = s[0]
+            if kind == "M":
+                return [n for x in s[1:] for n in needs(x)]
+            if kind == "Wm":
+                return [("Id",)]
             base = needs_bank.get(s, []) + ring.get(s, [])
             if kind == "Ls":
                 return [("Z",)]
             if kind == "Ci":
                 return [("Li",)]
             if kind == "T":
-                return base + [("Lr", s[1]), ("Id",)]
+                loads = [("Lr", s[1]), ("Lp", s[1] // 2), ("Lq",)]
+                return base + [[x for x in loads if x in queues[1]][0], ("Id",)]
             if kind == "CT":
                 return base + [("T", s[1])]
             if kind == "QT":
-                return [("CT", s[1])]
+                return [("CT", r) for r in GROUPS[s[1]]]
             if kind == "WP":
-                return [("Lw", s[1]), ("Ls",)]
+                return [("Lw", s[1]) if ("Lw", s[1]) in queues[1] else ("LW",), ("Ls",)]
             if kind == "WF":
-                return base + [("WP", s[2]), ("QT", s[1])]
+                return base + [("WP", s[2]), ("QT", GROUP_OF[s[1]][0])]
             if kind == "CW":
                 return [("WF",) + s[1:]]
             if kind == "QW":
-                return [("CW", 4 * s[1] + j, s[2]) for j in range(4)]
+                return [("CW", 4 * s[1] + j, h) for j in range(4) for h in range(2)]
             if kind == "I":
-                return [d_load(s[1])]
+                return [d_load(s[1])] + ([("QD", s[1] - 3)] if s[1] >= 3 else [])
             if kind == "QD":
-                return [("I", s[1], 0), ("I", s[1], 1)]
+                return [("I", s[1])]
             if kind == "G":
-                return base + [("QT", 8 + s[1])] + [("QD", UNITS.index((s[3], g, s[2]))) for g in range(2)]
+                return base + [("QT", GROUP_OF[8 + s[1]][0])] + [("QD", UNITS.index((s[3], g, s[2]))) for g in range(2)]
             if kind == "SC":
                 return base + [("G", s[1], s[2], 0), ("Ci",)]
             if kind == "ST":
@@ -169,13 +200,13 @@ def tile_lucas_kanade_flow_s11_kernel(tc, tmpl, dx, dy, inv, patch, win_words, w
             if kind == "CS":
                 return [("TS",) + s[1:]]
             if kind == "QS":
-                return [("CS",) + s[1:]]
+                return [("CS", s[1], h) for h in range(2)]
             if kind == "O":
-                return base + [("QS", s[1], 0), ("QS", s[1], 1), ("QW", s[3], 0), ("QW", s[3], 1)]
+                return base + [("QS", s[1]), ("QW", s[3])]
             if kind == "CO":
                 return base + [("O",) + s[1:]]
             if kind == "St":
-                return [("CO",) + s[1:]]
+                return [("CO",) + x[1:] for x in flat if x[0] == "O" and x[1 : len(s)] == s[1:]]
             return []
 
         def emit(s, engine):
@@ -192,15 +223,26 @@ def tile_lucas_kanade_flow_s11_kernel(tc, tmpl, dx, dy, inv, patch, win_words, w
                         out=ws_raw[32 * q : 32 * q + 4, :].bitcast(I32).rearrange("r (g n) -> r g n", g=2),
                         in_=win_scales[:, 4 * q : 4 * q + 4, :].rearrange("g r n -> r g n").bitcast(I32))
             elif kind == "Ci":
-                nc.vector.tensor_copy(out=inv_f[:], in_=inv_raw[:].rearrange("p a i -> p (a i)"))
+                nc.scalar.activation(out=inv_f[:], in_=inv_raw[:].rearrange("p a i -> p (a i)"), func=COPY)
             elif kind == "Lw":
                 h = s[1]
                 nc.sync.dma_start(out=w_raw[h][:].bitcast(I32).rearrange("p (g n) -> p g n", g=2),
                                   in_=win_words[:, :, 1024 * h : 1024 * (h + 1)].rearrange("g p b -> p g b").bitcast(I32))
             elif kind == "Lr":
                 r = s[1]
-                src = patch[128 * r : 128 * (r + 1), :] if r < 8 else tmpl_rows[:, r - 8, :]
-                nc.sync.dma_start(out=row_raw[r][:], in_=src)
+                src = patch_rows[r // 2][:, r % 2, :] if r < 8 else tmpl_rows[:, r - 8, :]
+                nc.sync.dma_start(out=row_raw[r], in_=src)
+            elif kind == "Lp":
+                x = s[1]
+                if x < 4:
+                    nc.sync.dma_start(out=patch_raw[x][:], in_=patch_rows[x])
+                else:
+                    nc.sync.dma_start(out=tmpl_raw[:, 2 * x - 8 : 2 * x - 6, :], in_=tmpl_rows[:, 2 * x - 8 : 2 * x - 6, :])
+            elif kind == "Lq":
+                nc.sync.dma_start(out=tmpl_raw[:], in_=tmpl_rows)
+            elif kind == "LW":
+                nc.sync.dma_start(out=w_all[:].bitcast(I32).rearrange("p (g n) -> p g n", g=2),
+                                  in_=win_words.rearrange("g p b -> p g b").bitcast(I32))
             elif kind == "LD":
                 a, g = s[1:]
                 raw = sb("d_raw%d%d" % (a, g), [128, 4, 1024], BF16)
@@ -215,60 +257,62 @@ def tile_lucas_kanade_flow_s11_kernel(tc, tmpl, dx, dy, inv, patch, win_words, w
                 nc.sync.dma_start(out=raw[:],
                                   in_=filters[a][512 * g : 512 * (g + 1), cols].rearrange("(p j) n -> p j n", j=4))
             elif kind == "T":
-                words = row_raw[s[1]][:].bitcast(F32)
+                words = row_raw[s[1]].bitcast(F32)
                 bank = bank_of[s][0]
                 for g in range(2):
                     for u in range(2):
                         j = 2 * g + u
                         nc.tensor.transpose(bank[:, 128 * j : 128 * (j + 1)], words[:, 256 * g + u : 256 * (g + 1) : 2], ident[:])
             elif kind == "CT":
-                live[s] = sb("row_t%d" % s[1], [128, 1024], BF16, ring="row_t", bufs=RING_ROW)
-                dst = live[s][:].bitcast(F32).rearrange("p (g r u) -> p g r u", g=2, u=2)
+                x, j = GROUP_OF[s[1]]
+                live["R", x] = row_t[used.index(x) % RING_ROW][:, : 1024 * len(GROUPS[x])]
+                dst = live["R", x][:, 1024 * j : 1024 * (j + 1)].bitcast(F32).rearrange("p (g r u) -> p g r u", g=2, u=2)
                 src = bank_of["T", s[1]][0][:].rearrange("p (g u r) -> p g r u", g=2, u=2)
                 if engine == 3:
                     nc.scalar.copy(out=dst, in_=src)
                 else:
                     nc.vector.tensor_copy(out=dst, in_=src)
             elif kind == "QT":
-                nc.vector.quantize_mx(out=row_codes[s[1]][:].bitcast(FP8X4), scales=row_scales[s[1]][:], in_=live["CT", s[1]][:])
+                nc.vector.quantize_mx(out=grp_codes[s[1]][:].bitcast(FP8X4), scales=grp_scales[s[1]][:], in_=live["R", s[1]])
             elif kind == "WP":
                 h = s[1]
-                for u in range(2):
-                    nc.vector.tensor_copy(
-                        out=w_scales[h, u][:].bitcast(I32).rearrange("p (g e b) -> p g e b", g=2, e=2),
-                        in_=ws_raw[:].bitcast(I32).rearrange("p (g h b e u) -> p h u g e b", g=2, h=2, e=2, u=2)[:, h, u])
-                    nc.vector.tensor_copy(
-                        out=w_codes[h, u][:].bitcast(I32).rearrange("p (g e b w) -> p g e b w", g=2, e=2, w=2),
-                        in_=w_raw[h][:].bitcast(I32).rearrange("p (g b e u w) -> p u g e b w", g=2, e=2, u=2, w=2)[:, u])
-            elif kind == "WF":
-                n, h = s[1:]
-                bank = bank_of[s][0]
-                for t in range(4):
-                    for g in range(2):
-                        u, x = t // 2, 2 * g + t % 2
+                nc.vector.tensor_copy(
+                    out=w_scales[h][:].bitcast(I32).rearrange("p (g f b) -> p g f b", g=2, f=4),
+                    in_=ws_raw[:].bitcast(I32).rearrange("p (g h b f) -> p h g f b", g=2, h=2, f=4)[:, h])
+                nc.vector.tensor_copy(
+                    out=w_codes[h][:].bitcast(I32).rearrange("p (g f b w) -> p g f b w", g=2, f=4, w=2),
+                    in_=w_view[h])
+            elif kind == "Wm":
+                for j in range(WARM):
+                    nc.tensor.transpose(banks[BANKS - 1][:, 128 * (j % 4) : 128 * (j % 4 + 1)], ident[:], ident[:])
+            elif kind == "WF" or kind == "M":
+                parts = s[1:] if kind == "M" else (s,)
+                for t, g, part in [(t, g, part) for t in range(4) for g in range(2) for part in parts]:
+                    if True:
+                        n, h = part[1:]
+                        x = 4 * g + 2 * (t % 2) + t // 2
                         nc.tensor.matmul_mx(
-                            out=bank[:, 128 * t : 128 * (t + 1)],
-                            lhsT=w_codes[h, u][:, 256 * x : 256 * (x + 1)].bitcast(FP4X4), lhsT_scale=w_scales[h, u][:, 128 * x : 128 * (x + 1)],
+                            out=bank_of[part][0][:, 128 * t : 128 * (t + 1)],
+                            lhsT=w_codes[h][:, 256 * x : 256 * (x + 1)].bitcast(FP4X4), lhsT_scale=w_scales[h][:, 128 * x : 128 * (x + 1)],
                             rhs=row_codes[n][:, 128 * g : 128 * (g + 1)].bitcast(FP8X4), rhs_scale=row_scales[n][:, 128 * g : 128 * (g + 1)],
                             start=(g == 0), stop=(g == 1))
             elif kind == "CW":
                 n, h = s[1:]
-                dst = wf_bf[n // 4, h][:, 512 * (n % 4) : 512 * (n % 4 + 1)].rearrange("p (r t) -> p r t", t=4)
+                dst = wf_bf[n // 4][:, 2048 * h + 512 * (n % 4) : 2048 * h + 512 * (n % 4 + 1)].rearrange("p (r t) -> p r t", t=4)
                 src = bank_of["WF", n, h][0][:].rearrange("p (t r) -> p r t", t=4)
                 if engine == 3:
                     nc.scalar.activation(out=dst, in_=src, func=COPY)
                 else:
                     nc.vector.tensor_copy(out=dst, in_=src)
             elif kind == "QW":
-                k = s[1:]
+                k = s[1]
                 nc.vector.quantize_mx(out=wf_codes[k][:].bitcast(FP8X4), scales=wf_scales[k][:], in_=wf_bf[k][:])
             elif kind == "I":
-                k, e = s[1:]
+                k = s[1]
                 a, g, h = UNITS[k]
-                if ("D", k) not in live:
-                    live["D", k] = sb("d_t%d" % k, [128, 2048], BF16, ring="d_t", bufs=3)
-                dst = live["D", k][:].rearrange("p (e u b i j) -> p e b u j i", e=2, u=2, i=4, j=4)[:, e]
-                src = live["raw", a, g, h].rearrange("p j (b e u i) -> p e b u j i", u=2, e=2, i=4)[:, e]
+                live["D", k] = d_t[k % 3]
+                dst = live["D", k][:].rearrange("p (f b i j) -> p b f j i", f=4, i=4, j=4)
+                src = live["raw", a, g, h].rearrange("p j (b f i) -> p b f j i", f=4, i=4)
                 if engine == 3:
                     nc.scalar.copy(out=dst, in_=src)
                 else:
@@ -308,34 +352,38 @@ def tile_lucas_kanade_flow_s11_kernel(tc, tmpl, dx, dy, inv, patch, win_words, w
                         nc.tensor.transpose(bank_of[s][0][:, 128 * j : 128 * (j + 1)], words[:, 128 * u : 128 * (u + 1)], ident[:])
             elif kind == "CS":
                 k = s[1:]
-                dst = sd_t[k][:].bitcast(F32).rearrange("p (c r u) -> p c r u", c=2, u=2)
+                dst = sd_t[k[0]][:, 1024 * k[1] : 1024 * (k[1] + 1)].bitcast(F32).rearrange("p (c r u) -> p c r u", c=2, u=2)
                 src = bank_of[("TS",) + k][0][:].rearrange("p (c u r) -> p c r u", c=2, u=2)
                 if engine == 3:
                     nc.scalar.copy(out=dst, in_=src)
                 else:
                     nc.vector.tensor_copy(out=dst, in_=src)
             elif kind == "QS":
-                k = s[1:]
+                k = s[1]
                 nc.vector.quantize_mx(out=sd_codes[k][:].bitcast(FP8X4), scales=sd_scales[k][:], in_=sd_t[k][:])
             elif kind == "O":
-                i, c, h = s[1:]
+                i, c, h = s[1:4]
+                lo, wide = (0, 512) if len(s) == 4 else (256 * s[4], 256)
                 for g in range(2):
                     nc.tensor.matmul_mx(
-                        out=bank_of[s][0][:],
-                        lhsT=sd_codes[i, g][:, 128 * c : 128 * (c + 1)].bitcast(FP8X4), lhsT_scale=sd_scales[i, g][:, 128 * c : 128 * (c + 1)],
-                        rhs=wf_codes[h, g][:].bitcast(FP8X4), rhs_scale=wf_scales[h, g][:],
+                        out=bank_of[s][0][:, :wide],
+                        lhsT=sd_codes[i][:, 256 * g + 128 * c : 256 * g + 128 * (c + 1)].bitcast(FP8X4),
+                        lhsT_scale=sd_scales[i][:, 256 * g + 128 * c : 256 * g + 128 * (c + 1)],
+                        rhs=wf_codes[h][:, 512 * g + lo : 512 * g + lo + wide].bitcast(FP8X4),
+                        rhs_scale=wf_scales[h][:, 512 * g + lo : 512 * g + lo + wide],
                         start=(g == 0), stop=(g == 1))
             elif kind == "CO":
-                i, c, h = s[1:]
-                live[s] = sb("res%d%d%d" % (i, c, h), [128, 512], F32, ring="res", bufs=RING_OUT)
-                dst = live[s][:]
+                lo, wide = (512 * s[3], 512) if len(s) == 4 else (512 * s[3] + 256 * s[4], 256)
+                dst = res[rows_out.index(s[1:3]) % RING_OUT][:, lo : lo + wide].rearrange("p (x r j) -> p x r j", r=128, j=2)
+                src = bank_of[("O",) + s[1:]][0][:, :wide].rearrange("p (x j r) -> p x r j", r=128, j=2)
                 if engine == 3:
-                    nc.scalar.copy(out=dst, in_=bank_of["O", i, c, h][0][:])
+                    nc.scalar.copy(out=dst, in_=src)
                 else:
-                    nc.vector.tensor_copy(out=dst, in_=bank_of["O", i, c, h][0][:])
+                    nc.vector.tensor_copy(out=dst, in_=src)
             elif kind == "St":
-                i, c, h = s[1:]
-                nc.sync.dma_start(out=out_rows[c][:, i, 512 * h : 512 * (h + 1)], in_=live["CO", i, c, h][:])
+                i, c = s[1:3]
+                lo, wide = (0, 1024) if len(s) == 3 else (512 * s[3], 512) if len(s) == 4 else (512 * s[3] + 256 * s[4], 256)
+                nc.sync.dma_start(out=out_rows[c][:, i, lo : lo + wide], in_=res[rows_out.index(s[1:3]) % RING_OUT][:, lo : lo + wide])
 
         done = set()
         at = [0] * len(queues)
@@ -346,5 +394,9 @@ def tile_lucas_kanade_flow_s11_kernel(tc, tmpl, dx, dy, inv, patch, win_words, w
                 while at[e] < len(queue) and all(n in done for n in needs(queue[at[e]])):
                     emit(queue[at[e]], e)
                     done.add(queue[at[e]])
+                    if queue[at[e]][0] == "M":
+                        for x in queue[at[e]][1:]:
+                            done.add(x)
+                            total += 1
                     at[e] += 1
             assert len(done) > before

@@ -22,43 +22,43 @@ WARM = 8
 UNITS = [(0, 0, 0), (0, 0, 1), (0, 1, 0), (0, 1, 1), (1, 0, 0), (1, 0, 1), (1, 1, 0), (1, 1, 1)]
 GROUPS = [(0,), (1,), (2, 3), (4, 5), (6, 7), (8, 9), (10, 11)]
 GROUP_OF = {r: (x, j) for x, rows in enumerate(GROUPS) for j, r in enumerate(rows)}
+RING_PP = 4
 RING_T = 6
 RING_ROW = 3
 RING_OUT = 5
 
 
 def orders():
-    sp = [("Lr", 0), ("Lr", 1), ("Lp", 1), ("Ls",), ("Lw", 0), ("Lw", 1), ("Li",), ("LD", 0, 0), ("Ld", 0, 1, 0),
-        ("Lp", 2), ("Lp", 3), ("Ld", 0, 1, 1), ("Lp", 5), ("Ld", 1, 0, 0), ("Lp", 4), ("Ld", 1, 1, 0), ("Ld", 1, 0, 1),
-        ("Ld", 1, 1, 1), ("St", 0, 0, 0), ("St", 0, 1, 0), ("St", 0, 0, 1), ("St", 0, 1, 1), ("St", 1, 0, 0), ("St", 1, 0, 1),
-        ("St", 1, 1, 1), ("St", 2, 0, 0), ("St", 1, 1, 0), ("St", 2, 0, 1), ("St", 2, 1, 0), ("St", 2, 1, 1), ("St", 3, 1, 0),
-        ("St", 3, 1, 1), ("St", 3, 0, 0), ("St", 3, 0, 1, 0), ("St", 3, 0, 1, 1)]
-    pe = [("Wm",), ("T", 0), ("T", 1), ("T", 3), ("T", 2), ("WF", 0, 0), ("WF", 0, 1), ("WF", 1, 0), ("M", ("WF", 2, 0),
-        ("WF", 3, 0)), ("WF", 1, 1), ("T", 4), ("T", 5), ("M", ("WF", 2, 1), ("WF", 3, 1)), ("T", 7), ("T", 6),
-        ("T", 10), ("M", ("WF", 4, 0), ("WF", 5, 0)), ("T", 9), ("T", 8), ("T", 11), ("M", ("WF", 4, 1), ("WF", 5, 1)),
-        ("M", ("WF", 6, 0), ("WF", 7, 0)), ("M", ("WF", 6, 1), ("WF", 7, 1)), ("G", 0, 0, 0), ("G", 0, 0, 1), ("G", 0, 1, 0),
-        ("G", 1, 1, 0), ("G", 0, 1, 1), ("G", 1, 1, 1), ("G", 1, 0, 0), ("G", 1, 0, 1), ("G", 2, 0, 0), ("TS", 0, 0),
-        ("TS", 0, 1), ("TS", 1, 1), ("G", 2, 1, 0), ("TS", 1, 0), ("G", 2, 0, 1), ("G", 3, 0, 0), ("G", 2, 1, 1),
-        ("O", 0, 0, 0), ("O", 0, 1, 0), ("O", 0, 0, 1), ("G", 3, 1, 0), ("O", 0, 1, 1), ("TS", 2, 0), ("TS", 2, 1),
-        ("G", 3, 0, 1), ("G", 3, 1, 1), ("O", 1, 0, 0), ("O", 1, 0, 1), ("O", 1, 1, 0), ("O", 1, 1, 1), ("O", 2, 0, 0),
-        ("TS", 3, 0), ("TS", 3, 1), ("O", 2, 0, 1), ("O", 2, 1, 0), ("O", 2, 1, 1), ("O", 3, 1, 0), ("O", 3, 1, 1),
-        ("O", 3, 0, 0), ("O", 3, 0, 1, 0), ("O", 3, 0, 1, 1)]
-    act = [("Ci",), ("CT", 1), ("CT", 2), ("CW", 0, 0), ("CW", 0, 1), ("CW", 1, 0), ("I", 2), ("CW", 2, 0), ("CT", 5),
-        ("CT", 4), ("CW", 1, 1), ("CW", 2, 1), ("CT", 7), ("CT", 6), ("CT", 10), ("CW", 3, 1), ("CW", 5, 0), ("CT", 9),
-        ("CT", 8), ("CW", 4, 0), ("CT", 11), ("CW", 5, 1), ("CW", 4, 1), ("CW", 7, 0), ("CW", 6, 0), ("CW", 7, 1),
-        ("SC", 0, 0, 0), ("CW", 6, 1), ("SC", 0, 0, 1), ("SC", 0, 1, 1), ("SC", 0, 1, 0), ("SC", 1, 1, 0), ("SC", 1, 1, 1),
-        ("SC", 1, 0, 1), ("SC", 1, 0, 0), ("CS", 0, 0), ("SC", 2, 0, 0), ("CS", 0, 1), ("SC", 2, 0, 1), ("CS", 1, 1),
-        ("SC", 2, 1, 1), ("SC", 2, 1, 0), ("CS", 1, 0), ("SC", 3, 0, 0), ("SC", 3, 0, 1), ("SC", 3, 1, 1), ("CO", 0, 1, 0),
-        ("CS", 2, 1), ("SC", 3, 1, 0), ("CS", 2, 0), ("CO", 0, 1, 1), ("CO", 1, 0, 0), ("CO", 1, 0, 1), ("CO", 1, 1, 1),
-        ("CO", 1, 1, 0), ("CS", 3, 0), ("CO", 2, 0, 1), ("CO", 2, 1, 0), ("CO", 2, 1, 1), ("CO", 3, 1, 1), ("CO", 3, 0, 0),
-        ("CO", 3, 0, 1, 1)]
-    vec = [("Z",), ("CT", 0), ("QT", 0), ("WP", 0), ("WP", 1), ("CT", 3), ("QT", 1), ("QT", 2), ("I", 1), ("I", 0),
-        ("QD", 1), ("CW", 3, 0), ("QD", 0), ("QD", 2), ("I", 3), ("QT", 3), ("QD", 3), ("I", 4), ("QT", 4), ("QD", 4),
-        ("I", 6), ("QT", 5), ("QD", 6), ("I", 5), ("I", 7), ("QD", 5), ("QD", 7), ("ST", 0, 0, 0), ("QT", 6), ("ST", 0, 0, 1),
-        ("ST", 0, 1, 1), ("ST", 0, 1, 0), ("ST", 1, 1, 0), ("ST", 1, 1, 1), ("ST", 1, 0, 1), ("ST", 1, 0, 0), ("QW", 0),
-        ("QS", 0), ("QW", 1), ("ST", 2, 0, 1), ("ST", 2, 1, 1), ("ST", 2, 0, 0), ("ST", 2, 1, 0), ("CO", 0, 0, 0),
-        ("CO", 0, 0, 1), ("QS", 1), ("ST", 3, 0, 0), ("ST", 3, 1, 1), ("QS", 2), ("ST", 3, 0, 1), ("ST", 3, 1, 0),
-        ("CO", 2, 0, 0), ("CS", 3, 1), ("QS", 3), ("CO", 3, 1, 0), ("CO", 3, 0, 1, 0)]
+    sp = [("Lr", 0), ("Lr", 1), ("LW",), ("Ls",), ("Lr", 2), ("LD", 0, 0), ("Lr", 3), ("Lr", 4), ("Lr", 6), ("Lr", 5),
+        ("Lr", 7), ("Li",), ("Ld", 0, 1, 0), ("Ld", 0, 1, 1), ("Lr", 8), ("Lr", 9), ("Ld", 1, 0, 0), ("Ld", 1, 0, 1),
+        ("LD", 1, 1), ("Lp", 5), ("St", 1, 0, 1), ("St", 1, 1, 0), ("St", 0, 1, 0), ("St", 0, 0), ("St", 0, 1, 1),
+        ("St", 1, 1, 1), ("St", 1, 0, 0), ("St", 2, 0, 0), ("St", 2, 0, 1), ("St", 2, 1, 0), ("St", 2, 1, 1), ("St", 3, 0, 1),
+        ("St", 3, 1, 0), ("St", 3, 1, 1), ("St", 3, 0, 0, 0), ("St", 3, 0, 0, 1)]
+    pe = [("T", 0), ("T", 1), ("WF", 0, 0), ("WF", 0, 1), ("T", 2), ("T", 3), ("T", 4), ("WF", 1, 1), ("T", 5),
+        ("T", 6), ("T", 7), ("WF", 3, 0), ("WF", 3, 1), ("WF", 4, 0), ("WF", 5, 1), ("WF", 2, 0), ("T", 8), ("T", 9),
+        ("WF", 2, 1), ("WF", 7, 1), ("WF", 1, 0), ("WF", 6, 0), ("WF", 6, 1), ("WF", 4, 1), ("G", 0, 0, 0), ("WF", 7, 0),
+        ("T", 10), ("T", 11), ("G", 1, 1, 0), ("G", 0, 0, 1), ("G", 1, 0, 1), ("G", 1, 0, 0), ("G", 1, 1, 1), ("G", 0, 1, 0),
+        ("G", 2, 0, 0), ("G", 0, 1, 1), ("WF", 5, 0), ("G", 2, 0, 1), ("G", 2, 1, 0), ("TS", 1, 0), ("TS", 0, 0),
+        ("TS", 0, 1), ("TS", 1, 1), ("G", 2, 1, 1), ("G", 3, 1, 0), ("G", 3, 0, 0), ("G", 3, 1, 1), ("O", 1, 1, 0),
+        ("G", 3, 0, 1), ("O", 1, 0, 1), ("O", 0, 0, 0), ("O", 0, 1, 0), ("O", 0, 0, 1), ("O", 0, 1, 1), ("TS", 2, 1),
+        ("TS", 2, 0), ("TS", 3, 0), ("TS", 3, 1), ("O", 1, 1, 1), ("O", 1, 0, 0), ("O", 2, 0, 0), ("O", 2, 0, 1),
+        ("O", 2, 1, 0), ("O", 2, 1, 1), ("O", 3, 0, 1), ("O", 3, 1, 0), ("O", 3, 1, 1), ("O", 3, 0, 0, 0), ("O", 3, 0, 0, 1)]
+    act = [("CW", 0, 0), ("CW", 0, 1), ("CT", 2), ("CT", 3), ("CT", 4), ("CW", 1, 1), ("CT", 5), ("CT", 7), ("CT", 6),
+        ("CW", 3, 0), ("CW", 3, 1), ("CW", 4, 0), ("CW", 5, 1), ("CW", 2, 0), ("CT", 8), ("CT", 9), ("CW", 2, 1),
+        ("CW", 7, 1), ("CW", 1, 0), ("CW", 6, 0), ("CW", 6, 1), ("CW", 4, 1), ("SC", 0, 0, 1), ("SC", 0, 0, 0),
+        ("CT", 10), ("CW", 7, 0), ("CT", 11), ("SC", 1, 1, 1), ("SC", 1, 1, 0), ("SC", 1, 0, 1), ("SC", 1, 0, 0),
+        ("SC", 0, 1, 1), ("SC", 0, 1, 0), ("SC", 2, 0, 1), ("SC", 2, 0, 0), ("CW", 5, 0), ("SC", 2, 1, 0), ("CS", 1, 0),
+        ("CS", 1, 1), ("SC", 2, 1, 1), ("CS", 0, 1), ("CS", 0, 0), ("SC", 3, 0, 1), ("SC", 3, 1, 1), ("SC", 3, 1, 0),
+        ("SC", 3, 0, 0), ("CO", 1, 0, 1), ("CO", 1, 1, 0), ("CO", 0, 1, 0), ("CO", 0, 0, 1), ("CS", 2, 1), ("CO", 0, 1, 1),
+        ("CO", 1, 1, 1), ("CS", 3, 0), ("CO", 2, 0, 0), ("CO", 2, 0, 1), ("CO", 2, 1, 0), ("CO", 2, 1, 1), ("CO", 3, 0, 1),
+        ("CO", 3, 1, 0), ("CO", 3, 1, 1), ("CO", 3, 0, 0, 1)]
+    vec = [("Z",), ("CT", 0), ("QT", 0), ("WP", 0), ("WP", 1), ("CT", 1), ("QT", 1), ("PP", 2), ("I", 0), ("I", 1),
+        ("PP", 6), ("QD", 0), ("QT", 2), ("QD", 1), ("QT", 3), ("Ci",), ("I", 2), ("QT", 4), ("I", 3), ("QD", 2),
+        ("QD", 3), ("I", 4), ("QT", 5), ("I", 5), ("QD", 4), ("I", 6), ("I", 7), ("QD", 6), ("QD", 7), ("QD", 5),
+        ("ST", 0, 0, 1), ("ST", 0, 0, 0), ("QT", 6), ("ST", 1, 1, 1), ("ST", 1, 1, 0), ("ST", 1, 0, 1), ("ST", 1, 0, 0),
+        ("ST", 0, 1, 0), ("ST", 0, 1, 1), ("QW", 0), ("ST", 2, 0, 0), ("ST", 2, 0, 1), ("QS", 1), ("ST", 2, 1, 0),
+        ("QW", 1), ("QS", 0), ("ST", 2, 1, 1), ("ST", 3, 1, 1), ("ST", 3, 0, 1), ("ST", 3, 1, 0), ("ST", 3, 0, 0),
+        ("CO", 0, 0, 0), ("CS", 2, 0), ("QS", 2), ("CO", 1, 0, 0), ("CS", 3, 1), ("QS", 3), ("CO", 3, 0, 0, 0)]
     return [[("Id",)], sp, pe, act, vec]
 
 
@@ -89,7 +89,7 @@ def tile_lucas_kanade_flow_s11_kernel(tc, tmpl, dx, dy, inv, patch, win_words, w
         patch_raw = [sb("patch_raw%d" % x, [128, 2, 1024], BF16) for x in range(4)]
         tmpl_raw = sb("tmpl_raw", [128, 4, 1024], BF16)
         row_raw = [patch_raw[r // 2][:, r % 2, :] if r < 8 else tmpl_raw[:, r - 8, :] for r in range(12)]
-        patch_rows = patch.rearrange("(x p j) k -> x p j k", x=4, j=2)
+        patch_rows = patch.rearrange("(x j p) k -> x p j k", x=4, j=2)
         grp_codes = [sb("row_codes%d" % x, [128, 256 * len(rows)], U32) for x, rows in enumerate(GROUPS)]
         grp_scales = [sb("row_scales%d" % x, [128, 256 * len(rows)], U8) for x, rows in enumerate(GROUPS)]
         row_codes = [grp_codes[GROUP_OF[r][0]][:, 256 * GROUP_OF[r][1] : 256 * (GROUP_OF[r][1] + 1)] for r in range(12)]
@@ -104,7 +104,7 @@ def tile_lucas_kanade_flow_s11_kernel(tc, tmpl, dx, dy, inv, patch, win_words, w
         sd_t = [sb("sd_t%d" % i, [128, 2048], BF16) for i in range(4)]
         sd_codes = [sb("sd_codes%d" % i, [128, 512], U32) for i in range(4)]
         sd_scales = [sb("sd_scales%d" % i, [128, 512], U8) for i in range(4)]
-        sd = {(i, s, c): sb("sd%d%d%d" % (i, s, c), [128, 512], BF16) for (i, s) in halves for c in range(2)}
+        sd = {(i, s, c): sb("sd%d%d%d" % (i, s, c), [128, 512], BF16) for i in range(2) for s in range(2) for c in range(2)}
         d_t = [sb("d_t%d" % k, [128, 2048], BF16) for k in range(3)]
         live = {}
         filters = (dx, dy)
@@ -144,6 +144,10 @@ def tile_lucas_kanade_flow_s11_kernel(tc, tmpl, dx, dy, inv, patch, win_words, w
                      ring_needs("SC", queues[3], RING_T, lambda s: ("ST",) + s[1:])):
             for key in part:
                 ring[key] = part[key]
+        turned = [s[1] for s in flat if s[0] == "T" and ("PP", s[1]) in queues[3] + queues[4]]
+        row_w = [sb("row_w%d" % k, [128, 512], F32) for k in range(RING_PP)]
+        for j in range(RING_PP, len(turned)):
+            ring["PP", turned[j]] = [("T", turned[j - RING_PP])]
         stores = [s for s in queues[1] if s[0] == "St"]
         res = [sb("res%d" % k, [128, 1024], F32) for k in range(RING_OUT)]
         rows_out = []
@@ -170,7 +174,9 @@ def tile_lucas_kanade_flow_s11_kernel(tc, tmpl, dx, dy, inv, patch, win_words, w
                 return [("Z",)]
             if kind == "Ci":
                 return [("Li",)]
-            if kind == "T":
+            if kind == "T" and s[1] in turned:
+                return base + [("PP", s[1]), ("Id",)]
+            if kind == "T" or kind == "PP":
                 loads = [("Lr", s[1]), ("Lp", s[1] // 2), ("Lq",)]
                 return base + [[x for x in loads if x in queues[1]][0], ("Id",)]
             if kind == "CT":
@@ -194,7 +200,7 @@ def tile_lucas_kanade_flow_s11_kernel(tc, tmpl, dx, dy, inv, patch, win_words, w
             if kind == "SC":
                 return base + [("G", s[1], s[2], 0), ("Ci",)]
             if kind == "ST":
-                return [("SC",) + s[1:], ("G", s[1], s[2], 1)]
+                return [("SC",) + s[1:], ("G", s[1], s[2], 1)] + ([("TS", s[1] - 2, s[2])] if s[1] >= 2 else [])
             if kind == "TS":
                 return base + [("ST",) + s[1:] + (c,) for c in range(2)]
             if kind == "CS":
@@ -223,7 +229,10 @@ def tile_lucas_kanade_flow_s11_kernel(tc, tmpl, dx, dy, inv, patch, win_words, w
                         out=ws_raw[32 * q : 32 * q + 4, :].bitcast(I32).rearrange("r (g n) -> r g n", g=2),
                         in_=win_scales[:, 4 * q : 4 * q + 4, :].rearrange("g r n -> r g n").bitcast(I32))
             elif kind == "Ci":
-                nc.scalar.activation(out=inv_f[:], in_=inv_raw[:].rearrange("p a i -> p (a i)"), func=COPY)
+                if engine == 3:
+                    nc.scalar.activation(out=inv_f[:], in_=inv_raw[:].rearrange("p a i -> p (a i)"), func=COPY)
+                else:
+                    nc.vector.tensor_copy(out=inv_f[:], in_=inv_raw[:].rearrange("p a i -> p (a i)"))
             elif kind == "Lw":
                 h = s[1]
                 nc.sync.dma_start(out=w_raw[h][:].bitcast(I32).rearrange("p (g n) -> p g n", g=2),
@@ -257,12 +266,22 @@ def tile_lucas_kanade_flow_s11_kernel(tc, tmpl, dx, dy, inv, patch, win_words, w
                 nc.sync.dma_start(out=raw[:],
                                   in_=filters[a][512 * g : 512 * (g + 1), cols].rearrange("(p j) n -> p j n", j=4))
             elif kind == "T":
-                words = row_raw[s[1]].bitcast(F32)
                 bank = bank_of[s][0]
                 for g in range(2):
                     for u in range(2):
                         j = 2 * g + u
-                        nc.tensor.transpose(bank[:, 128 * j : 128 * (j + 1)], words[:, 256 * g + u : 256 * (g + 1) : 2], ident[:])
+                        if s[1] in turned:
+                            words = row_w[turned.index(s[1]) % RING_PP][:, 128 * j : 128 * (j + 1)]
+                        else:
+                            words = row_raw[s[1]].bitcast(F32)[:, 256 * g + u : 256 * (g + 1) : 2]
+                        nc.tensor.transpose(bank[:, 128 * j : 128 * (j + 1)], words, ident[:])
+            elif kind == "PP":
+                dst = row_w[turned.index(s[1]) % RING_PP][:].rearrange("p (g u w) -> p g u w", g=2, u=2)
+                src = row_raw[s[1]].bitcast(F32).rearrange("p (g w u) -> p g u w", g=2, u=2)
+                if engine == 3:
+                    nc.scalar.copy(out=dst, in_=src)
+                else:
+                    nc.vector.tensor_copy(out=dst, in_=src)
             elif kind == "CT":
                 x, j = GROUP_OF[s[1]]
                 live["R", x] = row_t[used.index(x) % RING_ROW][:, : 1024 * len(GROUPS[x])]
@@ -339,14 +358,14 @@ def tile_lucas_kanade_flow_s11_kernel(tc, tmpl, dx, dy, inv, patch, win_words, w
             elif kind == "ST":
                 i, h, c = s[1:]
                 nc.vector.scalar_tensor_tensor(
-                    out=sd[i, h, c][:].rearrange("p (x e) -> p x e", e=2),
+                    out=sd[i % 2, h, c][:].rearrange("p (x e) -> p x e", e=2),
                     in0=bank_of["G", i, h, 1][0][:].rearrange("p (e x) -> p x e", e=2),
                     scalar=inv_f[:, 8 + 4 * c + i : 8 + 4 * c + i + 1],
                     in1=live["SC", i, h, c][:].rearrange("p (x e) -> p x e", e=2), op0=MULT, op1=ADD)
             elif kind == "TS":
                 i, h = s[1:]
                 for c in range(2):
-                    words = sd[i, h, c][:].bitcast(F32)
+                    words = sd[i % 2, h, c][:].bitcast(F32)
                     for u in range(2):
                         j = 2 * c + u
                         nc.tensor.transpose(bank_of[s][0][:, 128 * j : 128 * (j + 1)], words[:, 128 * u : 128 * (u + 1)], ident[:])
@@ -374,8 +393,8 @@ def tile_lucas_kanade_flow_s11_kernel(tc, tmpl, dx, dy, inv, patch, win_words, w
                         start=(g == 0), stop=(g == 1))
             elif kind == "CO":
                 lo, wide = (512 * s[3], 512) if len(s) == 4 else (512 * s[3] + 256 * s[4], 256)
-                dst = res[rows_out.index(s[1:3]) % RING_OUT][:, lo : lo + wide].rearrange("p (x r j) -> p x r j", r=128, j=2)
-                src = bank_of[("O",) + s[1:]][0][:, :wide].rearrange("p (x j r) -> p x r j", r=128, j=2)
+                dst = res[rows_out.index(s[1:3]) % RING_OUT][:, lo : lo + wide]
+                src = bank_of[("O",) + s[1:]][0][:, :wide]
                 if engine == 3:
                     nc.scalar.copy(out=dst, in_=src)
                 else:

from contextlib import ExitStack

import concourse.mybir as mybir
from concourse.masks import make_identity

M, N, Q, P, C = 512, 1024, 1024, 1024, 2
FLOPS = 2 * M * Q * P * 2 + 2 * N * Q * P + 2 * C * M * P * N

F32 = mybir.dt.float32
BF16 = mybir.dt.bfloat16
I32 = mybir.dt.int32
U32 = mybir.dt.uint32
U8 = mybir.dt.uint8
FP8X4 = mybir.dt.float8_e4m3fn_x4
FP4X4 = mybir.dt.float4_e2m1fn_x4
MULT = mybir.AluOpType.mult
ADD = mybir.AluOpType.add
COPY = mybir.ActivationFunctionType.Copy

BANKS = 8
WARM = 8
UNITS = [(0, 0, 0), (0, 0, 1), (0, 1, 0), (0, 1, 1), (1, 0, 0), (1, 0, 1), (1, 1, 0), (1, 1, 1)]
GROUPS = [(0,), (1,), (2, 3), (4, 5), (6, 7), (8, 9), (10, 11)]
GROUP_OF = {r: (x, j) for x, rows in enumerate(GROUPS) for j, r in enumerate(rows)}
RING_PP = 4
RING_T = 6
RING_ROW = 3
RING_OUT = 5


def orders():
    sp = [("Lr", 0), ("Lr", 1), ("LW",), ("Ls",), ("Lr", 2), ("LD", 0, 0), ("Lr", 3), ("Lr", 4), ("Lr", 6), ("Lr", 5),
        ("Lr", 7), ("Li",), ("Ld", 0, 1, 0), ("Ld", 0, 1, 1), ("Lr", 8), ("Lr", 9), ("Ld", 1, 0, 0), ("Ld", 1, 0, 1),
        ("LD", 1, 1), ("Lp", 5), ("St", 1, 0, 1), ("St", 1, 1, 0), ("St", 0, 1, 0), ("St", 0, 0), ("St", 0, 1, 1),
        ("St", 1, 1, 1), ("St", 1, 0, 0), ("St", 2, 0, 0), ("St", 2, 0, 1), ("St", 2, 1, 0), ("St", 2, 1, 1), ("St", 3, 0, 1),
        ("St", 3, 1, 0), ("St", 3, 1, 1), ("St", 3, 0, 0, 0), ("St", 3, 0, 0, 1)]
    pe = [("T", 0), ("T", 1), ("WF", 0, 0), ("WF", 0, 1), ("T", 2), ("T", 3), ("T", 4), ("WF", 1, 1), ("T", 5),
        ("T", 6), ("T", 7), ("WF", 3, 0), ("WF", 3, 1), ("WF", 4, 0), ("WF", 5, 1), ("WF", 2, 0), ("T", 8), ("T", 9),
        ("WF", 2, 1), ("WF", 7, 1), ("WF", 1, 0), ("WF", 6, 0), ("WF", 6, 1), ("WF", 4, 1), ("G", 0, 0, 0), ("WF", 7, 0),
        ("T", 10), ("T", 11), ("G", 1, 1, 0), ("G", 0, 0, 1), ("G", 1, 0, 1), ("G", 1, 0, 0), ("G", 1, 1, 1), ("G", 0, 1, 0),
        ("G", 2, 0, 0), ("G", 0, 1, 1), ("WF", 5, 0), ("G", 2, 0, 1), ("G", 2, 1, 0), ("TS", 1, 0), ("TS", 0, 0),
        ("TS", 0, 1), ("TS", 1, 1), ("G", 2, 1, 1), ("G", 3, 1, 0), ("G", 3, 0, 0), ("G", 3, 1, 1), ("O", 1, 1, 0),
        ("G", 3, 0, 1), ("O", 1, 0, 1), ("O", 0, 0, 0), ("O", 0, 1, 0), ("O", 0, 0, 1), ("O", 0, 1, 1), ("TS", 2, 1),
        ("TS", 2, 0), ("TS", 3, 0), ("TS", 3, 1), ("O", 1, 1, 1), ("O", 1, 0, 0), ("O", 2, 0, 0), ("O", 2, 0, 1),
        ("O", 2, 1, 0), ("O", 2, 1, 1), ("O", 3, 0, 1), ("O", 3, 1, 0), ("O", 3, 1, 1), ("O", 3, 0, 0, 0), ("O", 3, 0, 0, 1)]
    act = [("CW", 0, 0), ("CW", 0, 1), ("CT", 2), ("CT", 3), ("CT", 4), ("CW", 1, 1), ("CT", 5), ("CT", 7), ("CT", 6),
        ("CW", 3, 0), ("CW", 3, 1), ("CW", 4, 0), ("CW", 5, 1), ("CW", 2, 0), ("CT", 8), ("CT", 9), ("CW", 2, 1),
        ("CW", 7, 1), ("CW", 1, 0), ("CW", 6, 0), ("CW", 6, 1), ("CW", 4, 1), ("SC", 0, 0, 1), ("SC", 0, 0, 0),
        ("CT", 10), ("CW", 7, 0), ("CT", 11), ("SC", 1, 1, 1), ("SC", 1, 1, 0), ("SC", 1, 0, 1), ("SC", 1, 0, 0),
        ("SC", 0, 1, 1), ("SC", 0, 1, 0), ("SC", 2, 0, 1), ("SC", 2, 0, 0), ("CW", 5, 0), ("SC", 2, 1, 0), ("CS", 1, 0),
        ("CS", 1, 1), ("SC", 2, 1, 1), ("CS", 0, 1), ("CS", 0, 0), ("SC", 3, 0, 1), ("SC", 3, 1, 1), ("SC", 3, 1, 0),
        ("SC", 3, 0, 0), ("CO", 1, 0, 1), ("CO", 1, 1, 0), ("CO", 0, 1, 0), ("CO", 0, 0, 1), ("CS", 2, 1), ("CO", 0, 1, 1),
        ("CO", 1, 1, 1), ("CS", 3, 0), ("CO", 2, 0, 0), ("CO", 2, 0, 1), ("CO", 2, 1, 0), ("CO", 2, 1, 1), ("CO", 3, 0, 1),
        ("CO", 3, 1, 0), ("CO", 3, 1, 1), ("CO", 3, 0, 0, 1)]
    vec = [("Z",), ("CT", 0), ("QT", 0), ("WP", 0), ("WP", 1), ("CT", 1), ("QT", 1), ("PP", 2), ("I", 0), ("I", 1),
        ("PP", 6), ("QD", 0), ("QT", 2), ("QD", 1), ("QT", 3), ("Ci",), ("I", 2), ("QT", 4), ("I", 3), ("QD", 2),
        ("QD", 3), ("I", 4), ("QT", 5), ("I", 5), ("QD", 4), ("I", 6), ("I", 7), ("QD", 6), ("QD", 7), ("QD", 5),
        ("ST", 0, 0, 1), ("ST", 0, 0, 0), ("QT", 6), ("ST", 1, 1, 1), ("ST", 1, 1, 0), ("ST", 1, 0, 1), ("ST", 1, 0, 0),
        ("ST", 0, 1, 0), ("ST", 0, 1, 1), ("QW", 0), ("ST", 2, 0, 0), ("ST", 2, 0, 1), ("QS", 1), ("ST", 2, 1, 0),
        ("QW", 1), ("QS", 0), ("ST", 2, 1, 1), ("ST", 3, 1, 1), ("ST", 3, 0, 1), ("ST", 3, 1, 0), ("ST", 3, 0, 0),
        ("CO", 0, 0, 0), ("CS", 2, 0), ("QS", 2), ("CO", 1, 0, 0), ("CS", 3, 1), ("QS", 3), ("CO", 3, 0, 0, 0)]
    return [[("Id",)], sp, pe, act, vec]


def tile_lucas_kanade_flow_s11_kernel(tc, tmpl, dx, dy, inv, patch, win_words, win_scales, out):
    nc = tc.nc
    with ExitStack() as ctx:
        keep = ctx.enter_context(tc.tile_pool(name="keep", bufs=1))
        psum = ctx.enter_context(tc.psum_pool(name="psum", bufs=1))
        ctx.enter_context(tc.manual_schedule())

        def sb(name, shape, dtype, ring=None, bufs=1):
            return keep.tile(shape, dtype, name=name, tag=ring or name, bufs=bufs, align_bytes=64)

        banks = [psum.tile([128, 512], F32, name="bank%d" % b) for b in range(BANKS)]
        ident = sb("ident", [128, 128], F32)
        inv_raw = sb("inv_raw", [128, 4, 4], BF16)
        inv_f = sb("inv_f", [128, 16], F32)
        queues = orders()
        if ("LW",) in queues[1]:
            w_all = sb("w_all", [128, 4096], U8)
            w_view = [w_all[:].bitcast(I32).rearrange("p (g h b f w) -> p h g f b w", g=2, h=2, f=4, w=2)[:, h] for h in range(2)]
        else:
            w_raw = [sb("w_raw%d" % h, [128, 2048], U8) for h in range(2)]
            w_view = [w_raw[h][:].bitcast(I32).rearrange("p (g b f w) -> p g f b w", g=2, f=4, w=2) for h in range(2)]
        w_codes = [sb("w_codes%d" % h, [128, 2048], U8) for h in range(2)]
        ws_raw = sb("ws_raw", [128, 2048], U8)
        w_scales = [sb("w_scales%d" % h, [128, 1024], U8) for h in range(2)]
        patch_raw = [sb("patch_raw%d" % x, [128, 2, 1024], BF16) for x in range(4)]
        tmpl_raw = sb("tmpl_raw", [128, 4, 1024], BF16)
        row_raw = [patch_raw[r // 2][:, r % 2, :] if r < 8 else tmpl_raw[:, r - 8, :] for r in range(12)]
        patch_rows = patch.rearrange("(x j p) k -> x p j k", x=4, j=2)
        grp_codes = [sb("row_codes%d" % x, [128, 256 * len(rows)], U32) for x, rows in enumerate(GROUPS)]
        grp_scales = [sb("row_scales%d" % x, [128, 256 * len(rows)], U8) for x, rows in enumerate(GROUPS)]
        row_codes = [grp_codes[GROUP_OF[r][0]][:, 256 * GROUP_OF[r][1] : 256 * (GROUP_OF[r][1] + 1)] for r in range(12)]
        row_scales = [grp_scales[GROUP_OF[r][0]][:, 256 * GROUP_OF[r][1] : 256 * (GROUP_OF[r][1] + 1)] for r in range(12)]
        d_codes = {k: sb("d_codes%d%d%d" % k, [128, 512], U32) for k in UNITS}
        d_scales = {k: sb("d_scales%d%d%d" % k, [128, 512], U8) for k in UNITS}
        pairs = [(a, b) for a in range(2) for b in range(2)]
        wf_bf = [sb("wf_bf%d" % x, [128, 4096], BF16) for x in range(2)]
        wf_codes = [sb("wf_codes%d" % x, [128, 1024], U32) for x in range(2)]
        wf_scales = [sb("wf_scales%d" % x, [128, 1024], U8) for x in range(2)]
        halves = [(i, s) for i in range(4) for s in range(2)]
        sd_t = [sb("sd_t%d" % i, [128, 2048], BF16) for i in range(4)]
        sd_codes = [sb("sd_codes%d" % i, [128, 512], U32) for i in range(4)]
        sd_scales = [sb("sd_scales%d" % i, [128, 512], U8) for i in range(4)]
        sd = {(i, s, c): sb("sd%d%d%d" % (i, s, c), [128, 512], BF16) for i in range(2) for s in range(2) for c in range(2)}
        d_t = [sb("d_t%d" % k, [128, 2048], BF16) for k in range(3)]
        live = {}
        filters = (dx, dy)
        tmpl_rows = tmpl.rearrange("(p i) k -> p i k", i=4)
        out_rows = [out[c].rearrange("(p i) n -> p i n", i=4) for c in range(C)]

        queues = orders()
        bank_of = {}
        freed_by = {}
        needs_bank = {}
        turn = 0
        flat = [x for m in queues[2] for x in (m[1:] if m[0] == "M" else (m,)) if x[0] != "Wm"]
        for s in flat:
            if s[0] == "G":
                readers = [[("SC" if s[3] == 0 else "ST", s[1], s[2], c) for c in range(2)]]
            else:
                readers = [[({"T": "CT", "WF": "CW", "TS": "CS", "O": "CO"}[s[0]],) + s[1:]]]
            bank_of[s] = []
            needs_bank[s] = []
            for rd in readers:
                bank_of[s].append(banks[turn % BANKS])
                needs_bank[s] += freed_by.get(turn % BANKS, [])
                freed_by[turn % BANKS] = rd
                turn += 1

        def ring_needs(kind, queue, size, freer):
            mine = [s for s in queue if s[0] == kind]
            return {s: [freer(mine[j - size])] for j, s in enumerate(mine) if j >= size}

        used = []
        for s in flat:
            if s[0] == "T" and GROUP_OF[s[1]][0] not in used:
                used.append(GROUP_OF[s[1]][0])
        row_t = [sb("row_t%d" % k, [128, 2048], BF16) for k in range(RING_ROW)]
        ring = {}
        for part in ({("CT", r): [("QT", used[used.index(GROUP_OF[r][0]) - RING_ROW])] for r in range(12) if used.index(GROUP_OF[r][0]) >= RING_ROW},
                     ring_needs("SC", queues[3], RING_T, lambda s: ("ST",) + s[1:])):
            for key in part:
                ring[key] = part[key]
        turned = [s[1] for s in flat if s[0] == "T" and ("PP", s[1]) in queues[3] + queues[4]]
        row_w = [sb("row_w%d" % k, [128, 512], F32) for k in range(RING_PP)]
        for j in range(RING_PP, len(turned)):
            ring["PP", turned[j]] = [("T", turned[j - RING_PP])]
        stores = [s for s in queues[1] if s[0] == "St"]
        res = [sb("res%d" % k, [128, 1024], F32) for k in range(RING_OUT)]
        rows_out = []
        for s in flat:
            if s[0] == "O" and s[1:3] not in rows_out:
                rows_out.append(s[1:3])
        for s in flat:
            if s[0] == "O" and rows_out.index(s[1:3]) >= RING_OUT:
                old = rows_out[rows_out.index(s[1:3]) - RING_OUT]
                ring[("CO",) + s[1:]] = [x for x in stores if x[1:3] == old]

        def d_load(k):
            a, g, s = UNITS[k]
            return ("Ld", a, g, s) if ("Ld", a, g, s) in queues[1] else ("LD", a, g)

        def needs(s):
            kind = s[0]
            if kind == "M":
                return [n for x in s[1:] for n in needs(x)]
            if kind == "Wm":
                return [("Id",)]
            base = needs_bank.get(s, []) + ring.get(s, [])
            if kind == "Ls":
                return [("Z",)]
            if kind == "Ci":
                return [("Li",)]
            if kind == "T" and s[1] in turned:
                return base + [("PP", s[1]), ("Id",)]
            if kind == "T" or kind == "PP":
                loads = [("Lr", s[1]), ("Lp", s[1] // 2), ("Lq",)]
                return base + [[x for x in loads if x in queues[1]][0], ("Id",)]
            if kind == "CT":
                return base + [("T", s[1])]
            if kind == "QT":
                return [("CT", r) for r in GROUPS[s[1]]]
            if kind == "WP":
                return [("Lw", s[1]) if ("Lw", s[1]) in queues[1] else ("LW",), ("Ls",)]
            if kind == "WF":
                return base + [("WP", s[2]), ("QT", GROUP_OF[s[1]][0])]
            if kind == "CW":
                return [("WF",) + s[1:]]
            if kind == "QW":
                return [("CW", 4 * s[1] + j, h) for j in range(4) for h in range(2)]
            if kind == "I":
                return [d_load(s[1])] + ([("QD", s[1] - 3)] if s[1] >= 3 else [])
            if kind == "QD":
                return [("I", s[1])]
            if kind == "G":
                return base + [("QT", GROUP_OF[8 + s[1]][0])] + [("QD", UNITS.index((s[3], g, s[2]))) for g in range(2)]
            if kind == "SC":
                return base + [("G", s[1], s[2], 0), ("Ci",)]
            if kind == "ST":
                return [("SC",) + s[1:], ("G", s[1], s[2], 1)] + ([("TS", s[1] - 2, s[2])] if s[1] >= 2 else [])
            if kind == "TS":
                return base + [("ST",) + s[1:] + (c,) for c in range(2)]
            if kind == "CS":
                return [("TS",) + s[1:]]
            if kind == "QS":
                return [("CS", s[1], h) for h in range(2)]
            if kind == "O":
                return base + [("QS", s[1]), ("QW", s[3])]
            if kind == "CO":
                return base + [("O",) + s[1:]]
            if kind == "St":
                return [("CO",) + x[1:] for x in flat if x[0] == "O" and x[1 : len(s)] == s[1:]]
            return []

        def emit(s, engine):
            kind = s[0]
            if kind == "Z":
                nc.vector.memset(ws_raw[:].bitcast(I32), 0)
            elif kind == "Id":
                make_identity(nc, ident[:])
            elif kind == "Li":
                nc.sync.dma_start(out=inv_raw[:], in_=inv.rearrange("a c (p i) -> p (a c) i", i=4))
            elif kind == "Ls":
                for q in range(4):
                    nc.sync.dma_start(
                        out=ws_raw[32 * q : 32 * q + 4, :].bitcast(I32).rearrange("r (g n) -> r g n", g=2),
                        in_=win_scales[:, 4 * q : 4 * q + 4, :].rearrange("g r n -> r g n").bitcast(I32))
            elif kind == "Ci":
                if engine == 3:
                    nc.scalar.activation(out=inv_f[:], in_=inv_raw[:].rearrange("p a i -> p (a i)"), func=COPY)
                else:
                    nc.vector.tensor_copy(out=inv_f[:], in_=inv_raw[:].rearrange("p a i -> p (a i)"))
            elif kind == "Lw":
                h = s[1]
                nc.sync.dma_start(out=w_raw[h][:].bitcast(I32).rearrange("p (g n) -> p g n", g=2),
                                  in_=win_words[:, :, 1024 * h : 1024 * (h + 1)].rearrange("g p b -> p g b").bitcast(I32))
            elif kind == "Lr":
                r = s[1]
                src = patch_rows[r // 2][:, r % 2, :] if r < 8 else tmpl_rows[:, r - 8, :]
                nc.sync.dma_start(out=row_raw[r], in_=src)
            elif kind == "Lp":
                x = s[1]
                if x < 4:
                    nc.sync.dma_start(out=patch_raw[x][:], in_=patch_rows[x])
                else:
                    nc.sync.dma_start(out=tmpl_raw[:, 2 * x - 8 : 2 * x - 6, :], in_=tmpl_rows[:, 2 * x - 8 : 2 * x - 6, :])
            elif kind == "Lq":
                nc.sync.dma_start(out=tmpl_raw[:], in_=tmpl_rows)
            elif kind == "LW":
                nc.sync.dma_start(out=w_all[:].bitcast(I32).rearrange("p (g n) -> p g n", g=2),
                                  in_=win_words.rearrange("g p b -> p g b").bitcast(I32))
            elif kind == "LD":
                a, g = s[1:]
                raw = sb("d_raw%d%d" % (a, g), [128, 4, 1024], BF16)
                for h in range(2):
                    live["raw", a, g, h] = raw[:, :, 512 * h : 512 * (h + 1)]
                nc.sync.dma_start(out=raw[:], in_=filters[a][512 * g : 512 * (g + 1), :].rearrange("(p j) n -> p j n", j=4))
            elif kind == "Ld":
                a, g, h = s[1:]
                cols = slice(512 * h, 512 * (h + 1))
                raw = sb("d_raw%d%d%d" % (a, g, h), [128, 4, 512], BF16)
                live["raw", a, g, h] = raw[:]
                nc.sync.dma_start(out=raw[:],
                                  in_=filters[a][512 * g : 512 * (g + 1), cols].rearrange("(p j) n -> p j n", j=4))
            elif kind == "T":
                bank = bank_of[s][0]
                for g in range(2):
                    for u in range(2):
                        j = 2 * g + u
                        if s[1] in turned:
                            words = row_w[turned.index(s[1]) % RING_PP][:, 128 * j : 128 * (j + 1)]
                        else:
                            words = row_raw[s[1]].bitcast(F32)[:, 256 * g + u : 256 * (g + 1) : 2]
                        nc.tensor.transpose(bank[:, 128 * j : 128 * (j + 1)], words, ident[:])
            elif kind == "PP":
                dst = row_w[turned.index(s[1]) % RING_PP][:].rearrange("p (g u w) -> p g u w", g=2, u=2)
                src = row_raw[s[1]].bitcast(F32).rearrange("p (g w u) -> p g u w", g=2, u=2)
                if engine == 3:
                    nc.scalar.copy(out=dst, in_=src)
                else:
                    nc.vector.tensor_copy(out=dst, in_=src)
            elif kind == "CT":
                x, j = GROUP_OF[s[1]]
                live["R", x] = row_t[used.index(x) % RING_ROW][:, : 1024 * len(GROUPS[x])]
                dst = live["R", x][:, 1024 * j : 1024 * (j + 1)].bitcast(F32).rearrange("p (g r u) -> p g r u", g=2, u=2)
                src = bank_of["T", s[1]][0][:].rearrange("p (g u r) -> p g r u", g=2, u=2)
                if engine == 3:
                    nc.scalar.copy(out=dst, in_=src)
                else:
                    nc.vector.tensor_copy(out=dst, in_=src)
            elif kind == "QT":
                nc.vector.quantize_mx(out=grp_codes[s[1]][:].bitcast(FP8X4), scales=grp_scales[s[1]][:], in_=live["R", s[1]])
            elif kind == "WP":
                h = s[1]
                nc.vector.tensor_copy(
                    out=w_scales[h][:].bitcast(I32).rearrange("p (g f b) -> p g f b", g=2, f=4),
                    in_=ws_raw[:].bitcast(I32).rearrange("p (g h b f) -> p h g f b", g=2, h=2, f=4)[:, h])
                nc.vector.tensor_copy(
                    out=w_codes[h][:].bitcast(I32).rearrange("p (g f b w) -> p g f b w", g=2, f=4, w=2),
                    in_=w_view[h])
            elif kind == "Wm":
                for j in range(WARM):
                    nc.tensor.transpose(banks[BANKS - 1][:, 128 * (j % 4) : 128 * (j % 4 + 1)], ident[:], ident[:])
            elif kind == "WF" or kind == "M":
                parts = s[1:] if kind == "M" else (s,)
                for t, g, part in [(t, g, part) for t in range(4) for g in range(2) for part in parts]:
                    if True:
                        n, h = part[1:]
                        x = 4 * g + 2 * (t % 2) + t // 2
                        nc.tensor.matmul_mx(
                            out=bank_of[part][0][:, 128 * t : 128 * (t + 1)],
                            lhsT=w_codes[h][:, 256 * x : 256 * (x + 1)].bitcast(FP4X4), lhsT_scale=w_scales[h][:, 128 * x : 128 * (x + 1)],
                            rhs=row_codes[n][:, 128 * g : 128 * (g + 1)].bitcast(FP8X4), rhs_scale=row_scales[n][:, 128 * g : 128 * (g + 1)],
                            start=(g == 0), stop=(g == 1))
            elif kind == "CW":
                n, h = s[1:]
                dst = wf_bf[n // 4][:, 2048 * h + 512 * (n % 4) : 2048 * h + 512 * (n % 4 + 1)].rearrange("p (r t) -> p r t", t=4)
                src = bank_of["WF", n, h][0][:].rearrange("p (t r) -> p r t", t=4)
                if engine == 3:
                    nc.scalar.activation(out=dst, in_=src, func=COPY)
                else:
                    nc.vector.tensor_copy(out=dst, in_=src)
            elif kind == "QW":
                k = s[1]
                nc.vector.quantize_mx(out=wf_codes[k][:].bitcast(FP8X4), scales=wf_scales[k][:], in_=wf_bf[k][:])
            elif kind == "I":
                k = s[1]
                a, g, h = UNITS[k]
                live["D", k] = d_t[k % 3]
                dst = live["D", k][:].rearrange("p (f b i j) -> p b f j i", f=4, i=4, j=4)
                src = live["raw", a, g, h].rearrange("p j (b f i) -> p b f j i", f=4, i=4)
                if engine == 3:
                    nc.scalar.copy(out=dst, in_=src)
                else:
                    nc.vector.tensor_copy(out=dst, in_=src)
            elif kind == "QD":
                k = UNITS[s[1]]
                nc.vector.quantize_mx(out=d_codes[k][:].bitcast(FP8X4), scales=d_scales[k][:], in_=live["D", s[1]][:])
            elif kind == "G":
                i, h, a = s[1:]
                if True:
                    for g in range(2):
                        nc.tensor.matmul_mx(
                            out=bank_of[s][0][:],
                            lhsT=row_codes[8 + i][:, 128 * g : 128 * (g + 1)].bitcast(FP8X4),
                            lhsT_scale=row_scales[8 + i][:, 128 * g : 128 * (g + 1)],
                            rhs=d_codes[a, g, h][:].bitcast(FP8X4), rhs_scale=d_scales[a, g, h][:],
                            start=(g == 0), stop=(g == 1))
            elif kind == "SC":
                i, h, c = s[1:]
                live[s] = sb("gx_part%d%d%d" % s[1:], [128, 512], F32, ring="gx_part", bufs=RING_T)
                nc.scalar.activation(out=live[s][:].rearrange("p (x e) -> p x e", e=2),
                                     in_=bank_of["G", i, h, 0][0][:].rearrange("p (e x) -> p x e", e=2),
                                     func=COPY, scale=inv_f[:, 4 * c + i : 4 * c + i + 1])
            elif kind == "ST":
                i, h, c = s[1:]
                nc.vector.scalar_tensor_tensor(
                    out=sd[i % 2, h, c][:].rearrange("p (x e) -> p x e", e=2),
                    in0=bank_of["G", i, h, 1][0][:].rearrange("p (e x) -> p x e", e=2),
                    scalar=inv_f[:, 8 + 4 * c + i : 8 + 4 * c + i + 1],
                    in1=live["SC", i, h, c][:].rearrange("p (x e) -> p x e", e=2), op0=MULT, op1=ADD)
            elif kind == "TS":
                i, h = s[1:]
                for c in range(2):
                    words = sd[i % 2, h, c][:].bitcast(F32)
                    for u in range(2):
                        j = 2 * c + u
                        nc.tensor.transpose(bank_of[s][0][:, 128 * j : 128 * (j + 1)], words[:, 128 * u : 128 * (u + 1)], ident[:])
            elif kind == "CS":
                k = s[1:]
                dst = sd_t[k[0]][:, 1024 * k[1] : 1024 * (k[1] + 1)].bitcast(F32).rearrange("p (c r u) -> p c r u", c=2, u=2)
                src = bank_of[("TS",) + k][0][:].rearrange("p (c u r) -> p c r u", c=2, u=2)
                if engine == 3:
                    nc.scalar.copy(out=dst, in_=src)
                else:
                    nc.vector.tensor_copy(out=dst, in_=src)
            elif kind == "QS":
                k = s[1]
                nc.vector.quantize_mx(out=sd_codes[k][:].bitcast(FP8X4), scales=sd_scales[k][:], in_=sd_t[k][:])
            elif kind == "O":
                i, c, h = s[1:4]
                lo, wide = (0, 512) if len(s) == 4 else (256 * s[4], 256)
                for g in range(2):
                    nc.tensor.matmul_mx(
                        out=bank_of[s][0][:, :wide],
                        lhsT=sd_codes[i][:, 256 * g + 128 * c : 256 * g + 128 * (c + 1)].bitcast(FP8X4),
                        lhsT_scale=sd_scales[i][:, 256 * g + 128 * c : 256 * g + 128 * (c + 1)],
                        rhs=wf_codes[h][:, 512 * g + lo : 512 * g + lo + wide].bitcast(FP8X4),
                        rhs_scale=wf_scales[h][:, 512 * g + lo : 512 * g + lo + wide],
                        start=(g == 0), stop=(g == 1))
            elif kind == "CO":
                lo, wide = (512 * s[3], 512) if len(s) == 4 else (512 * s[3] + 256 * s[4], 256)
                dst = res[rows_out.index(s[1:3]) % RING_OUT][:, lo : lo + wide]
                src = bank_of[("O",) + s[1:]][0][:, :wide]
                if engine == 3:
                    nc.scalar.copy(out=dst, in_=src)
                else:
                    nc.vector.tensor_copy(out=dst, in_=src)
            elif kind == "St":
                i, c = s[1:3]
                lo, wide = (0, 1024) if len(s) == 3 else (512 * s[3], 512) if len(s) == 4 else (512 * s[3] + 256 * s[4], 256)
                nc.sync.dma_start(out=out_rows[c][:, i, lo : lo + wide], in_=res[rows_out.index(s[1:3]) % RING_OUT][:, lo : lo + wide])

        done = set()
        at = [0] * len(queues)
        total = sum(len(q) for q in queues)
        while len(done) < total:
            before = len(done)
            for e, queue in enumerate(queues):
                while at[e] < len(queue) and all(n in done for n in needs(queue[at[e]])):
                    emit(queue[at[e]], e)
                    done.add(queue[at[e]])
                    if queue[at[e]][0] == "M":
                        for x in queue[at[e]][1:]:
                            done.add(x)
                            total += 1
                    at[e] += 1
            assert len(done) > before
